import numpy as np, ml_dtypes
CORES = [3,11,19,27,35,43,51,59]
N = 8
import mx_ref
BF = ml_dtypes.bfloat16
def gcols(t, e):
    v = np.concatenate([t.reshape(8, 16, -1, 4), np.zeros((8, 16, 1, 4), BF)], axis=2)
    return np.ascontiguousarray(np.stack([v[g][:, e[g]] for g in range(8)])).reshape(128, -1)
def tile(rs):
    return np.stack(rs, axis=2).reshape(128, -1).astype(BF)
def pick(q, e):
    c = np.concatenate([q[0].reshape(128, -1, 4), np.zeros((128, 1, 4), np.uint8)], axis=1); s = np.concatenate([q[1], np.ones((16, 1), np.uint8)], axis=1)
    return (np.ascontiguousarray(c[:, e].reshape(128, -1)), np.ascontiguousarray(s[:, e]))
def join(*qs):
    return (np.concatenate([q[0] for q in qs], axis=1), np.concatenate([q[1] for q in qs], axis=1))
def put(q, e, v):
    c, s = q[0].reshape(128, -1, 4).copy(), q[1].copy(); c[:, e] = v[0].reshape(128, -1, 4); s[:, e] = v[1]
    return (c.reshape(128, -1), s)
def pk(c, s):
    return (np.ascontiguousarray(c), mx_ref.live(s))
def emit(q):
    return q[0], q[1]
def packed(v, rng):
    q = [mx_ref.quantize(np.ascontiguousarray(v[r])) for r in range(N)]
    return np.stack([a for a, b in q]), np.stack([mx_ref.plane(b, rng) for a, b in q])
def values_of_codes():
    e, c = np.zeros((128, 128, 4), np.float32), np.zeros((128, 2, 4), np.uint8)
    e[np.arange(128), np.arange(128), 0] = 1
    c[:127, :, 0] = np.arange(256).reshape(2, 128).T[:127]
    return mx_ref.matmul(mx_ref.quantize(e.reshape(128, 512).astype(BF)), (c.reshape(128, 8), np.full((16, 2), 127, np.uint8))).T.reshape(-1).astype(np.float64)
CODE_VALUE, SCALE_VALUE = values_of_codes(), 2.0 ** (np.arange(256) - 127.0)
def decode(q):
    return (CODE_VALUE[q[0]].reshape(16, 8, -1, 4) * SCALE_VALUE[q[1]][:, None, :, None] + 0.0).reshape(128, -1).astype(np.float32)
def f(rng, *shape):
    return mx_ref.flush((rng.standard_normal(shape, dtype=np.float32) * np.exp2(rng.integers(-2, 3, shape[:-1] + (1,)))).astype(BF))
def wide(rng, *shape, cols=0):
    v = rng.standard_normal(shape, dtype=np.float32) * np.exp2(rng.integers(-12, 13, shape)).astype(np.float32)
    if cols: v *= np.repeat(np.exp2(rng.integers(-cols, cols + 1, shape[:-2] + (1, shape[-1] // 4))) * (rng.random(shape[:-2] + (1, shape[-1] // 4)) > 0.0625), 4, axis=-1).astype(np.float32)
    return mx_ref.flush(v.astype(BF))
C, S = 512, 64
def order(p):
    return np.argsort(-(p[::16] + np.float32(0.0)), axis=1, kind="stable")
def places(o):
    return np.argsort(o, axis=1)
def numbers_of(rng):
    return {"x": np.array(f(rng, N, 128, 4 * C)), "u": np.array(f(rng, N, 128, 512)), "v": np.array(f(rng, N, 128, 512)), "m": np.array(f(rng, N, 128, 512))}
def weights(rng, w):
    c, p = packed(w, rng)
    return {"wc": c, "ws": p}
def unit(rng, a, b, low=False):
    w = np.zeros((N, 128, 4, 128, 4), np.float32)
    i = np.arange(128)
    j = i[i % 16 // 4 == 2]
    for k in range(4):
        w[:, i, k, i, k] = np.where(i % 16 < 8, a, b)
        if low: w[:, j + 4, k, j, k] = b
    return weights(rng, w.reshape(N, 128, 2048).astype(BF))
def signs(rng):
    return np.stack([rng.permutation(8) % 2 * 2.0 - 1.0 for r in range(N)])
def digits(s):
    return np.stack([s // 64 * 64, s // 8 % 8 * 8, s % 8, 0 * s], axis=-1)
def setup_inputs(rng):
    return {**numbers_of(rng), **weights(rng, f(rng, N, 128, 2048))}
def setup_inputs_ties(rng):
    d = numbers_of(rng)
    e = rng.permutation(N)
    x = d["x"].reshape(N, 8, 16, C, 4)
    for r in range(N):
        k = np.zeros(C, int) if r == e[0] else rng.permutation(C) % 3
        a = np.abs(x[r][:, :8, :3].astype(np.float32))
        a[:, :, 2] = 0
        x[r][:, :8] = a[:, :, k].astype(BF)
        if r == e[2]:
            z = np.flatnonzero(k == 2)
            n = int(rng.integers(0, len(z) - 15))
            x[r][:, :, z[n:n + 16]] = 0
    x[e[1]][:, :8] = x[e[0]][:, :8]
    u, v = d["u"].reshape(N, 8, 16, 128, 4), d["v"].reshape(N, 8, 16, 128, 4)
    u[:, :, 8:, ::16] = 0
    v[:, :, 8:, ::16] = 0
    w = np.array(f(rng, N, 128, 2048)).astype(np.float32).reshape(N, 8, 16, 4, 8, 16, 4)
    w[:, :, 8:, :, :, :8] = 0
    w[:, :, :8, :, :, 8:] = 0
    w[:, :, :8, :, :, :8] = 0.0 - np.abs(w[:, :, :8, :, :, :8])
    return {"x": x.reshape(N, 128, 4 * C), "u": u.reshape(N, 128, 512), "v": v.reshape(N, 128, 512), "m": d["m"], **weights(rng, w.reshape(N, 128, 2048).astype(BF))}
def setup_inputs_near(rng):
    d = numbers_of(rng)
    x = d["x"].astype(np.float32).reshape(N, 8, 16, C, 4)
    s = (np.arange(C) // 2 + rng.integers(0, C // 2, (N, 8, 1))) % (C // 2)
    g = ((s[..., None] >> np.arange(8)) & 1) * np.exp2(np.arange(8) - 23.0)
    x[:, :, 0] = 0
    x[:, :, 0, :, 0] = -1
    x[:, :, 8] = 0.0 - g[..., :4]
    x[:, :, 9] = 0.0 - g[..., 4:]
    x[:, :, 10:] = rng.integers(4, 8, (N, 8, 6, C, 4)) * rng.choice([-1.0, 1.0], (N, 8, 6, C, 4)) * 2.0 ** -20
    x = x * np.float32(2.0 ** 16)
    u, v = d["u"].reshape(N, 128, 128, 4), d["v"].reshape(N, 128, 128, 4)
    u[:, :, ::16] = 0
    v[:, :, ::16] = 0
    a, b = (signs(rng) * -2.0 ** -30).astype(np.float32).astype(BF), (signs(rng) * -2.0 ** -30).astype(np.float32).astype(BF)
    for h in range(0, 128, 16):
        u[:, h, h, 0] = a[:, h // 16]
        v[:, h, h, 0] = b[:, h // 16]
        u[:, h + 8:h + 10, h] = -2.0 ** -30
        v[:, h + 8:h + 10, h] = 2.0 ** -30
    return {"x": x.reshape(N, 128, 4 * C).astype(BF), "u": u.reshape(N, 128, 512), "v": v.reshape(N, 128, 512), "m": d["m"], **unit(rng, 256, 256)}
def setup_inputs_huge(rng):
    d = numbers_of(rng)
    x = np.zeros((N, 8, 16, C, 4))
    e = rng.permutation(N)
    one = rng.permutation(N) < N // 2
    both = rng.permutation(N // 2) % 2
    for r in range(N):
        s = np.ones(N) if one[r] else rng.permutation(N) % 2 * 2.0 - 1.0
        val = np.sort(np.r_[0.875, 1 + 0.125 * np.arange(N - 1)] * 2.0 ** 29 * s)[::-1]
        lev = rng.permutation(C) % N
        x[r][:, :8] = val[lev][:, None]
        x[r][:, 8:] = 2.0 ** 13 * (0.5 + 0.5 * rng.random((8, 8, C, 4)))
        h = np.sort(rng.permutation(S)[:2])
        for l in range(N):
            j = np.flatnonzero(lev == l)[h]
            k = both[min(l, N - 1 - l)]
            if r == e[0]: x[r][:, 8:, j] = np.array([1.75, 1.625] if k else [1.625, 1.75])[:, None] * 2.0 ** 24
            if r == e[1] and k: x[r][:, 8:, j[0]] = -1.625 * 2.0 ** 24
    u, v = d["u"].reshape(N, 8, 16, 128, 4), d["v"].reshape(N, 8, 16, 128, 4)
    for t, p in ((u, slice(0, 8)), (v, slice(8, 16))):
        a = 2.0 ** 30 * (1 - 0.125 * rng.random((N, 8, 8, 8, 4))) * signs(rng)[:, None, None, :, None]
        t[:, :, :, ::16] = 0
        t[:, :, p, ::16] = a.astype(np.float32).astype(BF)
    return {"x": x.astype(np.float32).reshape(N, 128, 4 * C).astype(BF), "u": u.reshape(N, 128, 512), "v": v.reshape(N, 128, 512), "m": d["m"], **unit(rng, 0.015625, 4096)}
def setup_inputs_scan(rng):
    d = numbers_of(rng)
    i = np.arange(C)
    a = rng.integers(1, 26, (N, 8, 1))
    at = a + 26 * rng.integers(0, (C - 93) // 26 + 1, (N, 8, 1))
    two = np.stack([rng.permutation(8) < 2 for r in range(N)])[..., None]
    far = two & (i >= at) & (i < at + 68)
    n = np.where(two & (i >= at + 68), i - at - 68, i - a)
    since = np.where(far, i - at, np.where(i < a, i, n % 26))
    anew = far & (since == 40)
    quiet = (i >= a) & (n // 26 % 2 == 1)
    shape = (N, 8, C, 4, 4)
    kind = rng.choice(5, shape, p=[0.2, 0.1, 0.2, 0.35, 0.15])
    kind = np.where(quiet[..., None, None] & (kind < 3), 3, kind)
    kind = np.where(far[..., None, None], 4, kind)
    kind = np.where((since == 0)[..., None, None], 5, kind)
    kind[..., 3] = np.where(anew[..., None], 5, kind[..., 3])
    top = 16 * rng.integers(8, 13, shape) + rng.integers(7, 10, shape)
    rest = rng.integers(128, 240, shape)
    h, now = np.zeros(shape, int), np.zeros((N, 8, 4, 4), int)
    for k in range(C):
        t = kind[:, :, k]
        now = np.where(t == 5, top[:, :, k], now)
        h[:, :, k] = np.select([t == 0, t == 1, t == 2, t == 3, t == 5], [now - 1, now + 1, rest[:, :, k], -rest[:, :, k], now], 0)
        now = now + (t == 1)
    head = far & (since == 0) | anew
    size = np.where(head, np.where(anew, 2.0 ** -7, 2.0 ** 21), np.exp2(5.0 - since))[..., None, None] * np.where(kind == 2, 0.0625, 1.0)
    high = np.sign(h) * (np.abs(h) // 16 * 16)
    upper = np.where(head[..., None, None], h - high, high)
    w = np.argsort(rng.random((N, 8, C)), axis=2)
    g = np.arange(8)[:, None]
    c = S * np.arange(N)[:, None, None] + w % S
    p = np.concatenate([0.0 - digits(C - 1 - c)[..., None, :], 0.0 - digits(C - 1 - i + 0 * c)[..., None, :], upper * size, (h - upper) * size], axis=3)
    q, z = np.zeros(p.shape), np.zeros(p.shape)
    q[w // S, g, c] = p
    z[np.arange(N)[:, None, None], g, np.argsort(rng.random((N, 8, C)), axis=2)] = q
    x = d["x"].astype(np.float32).reshape(N, 8, 16, C, 4)
    x[:, :, np.r_[0:2, 8:16]] = z.transpose(0, 1, 3, 2, 4)
    u, v = d["u"].reshape(N, 128, 128, 4), d["v"].reshape(N, 128, 128, 4)
    u[:, :, ::16] = 0
    v[:, :, ::16] = 0
    for b in range(0, 128, 16):
        u[:, b, b, :3] = -1
        v[:, b + 1, b, :3] = -1
    return {"x": x.reshape(N, 128, 4 * C).astype(BF), "u": u.reshape(N, 128, 512), "v": v.reshape(N, 128, 512), "m": d["m"], **unit(rng, 256, 256, True)}
def setup_inputs_spread(rng):
    d = setup_inputs(rng)
    x = wide(rng, N, 128, 4 * C).astype(np.float32).reshape(N, 128, C, 4)
    x = x * np.exp2(rng.integers(-6, 7, (N, 1, C, 1))).astype(np.float32)
    for r in range(N): x[r][:, rng.permutation(C)[:24 // N]] = 0
    d["x"] = mx_ref.flush(x.reshape(N, 128, 4 * C).astype(BF))
    return d
def scanned(x, u, v, wc, ws):
    first, second, out, value = [], [], [], []
    run = np.arange(S)
    for r in range(N):
        o = order(mx_ref.matmul(mx_ref.quantize(u[r]), mx_ref.quantize(x[r])))
        first.append(o)
        out.append(mx_ref.quantize(gcols(x[r], o)))
    for d in range(N):
        w = pk(wc[d], ws[d])
        a = join(*[pick(out[r], S * d + run) for r in range(N)])
        h = tile([mx_ref.matmul(pick(w, np.arange(128 * b, 128 * b + 128)), a) * np.float32(0.00390625) for b in range(4)])
        o = order(mx_ref.matmul(mx_ref.quantize(v[d]), mx_ref.quantize(h)))
        second.append(o)
        s = gcols(h, o).astype(np.float32).reshape(128, C, 4)
        s[:, 0] = np.maximum(s[:, 0], np.float32(0.0))
        for i in range(1, C): s[:, i] = np.maximum(s[:, i - 1] * np.float32(0.5), s[:, i])
        value.append(s + np.float32(0.0))
    return first, second, value
def check_inputs(d):
    b = []
    for k in ("x", "u", "v", "m"):
        a = np.abs(d[k].astype(np.float32))
        if not (np.isfinite(a).all() and ((a == 0) | (a >= 2.0 ** -30) & (a <= 2.0 ** 30)).all()): b.append("a value of " + k)
    return b
def reference(x, u, v, m, wc, ws):
    first, second, value = scanned(x, u, v, wc, ws)
    back = [mx_ref.quantize(gcols(value[d].reshape(128, 4 * C).astype(BF), places(second[d]))) for d in range(N)]
    run = np.arange(S)
    y, oa, ob = np.zeros((N, 128, C), np.float32), np.zeros((N, 8, C), np.float32), np.zeros((N, 8, C), np.float32)
    oc, osc = np.zeros((N, 128, 4 * C), np.uint8), np.zeros((N, 16, C), np.uint8)
    for r in range(N):
        b = decode(join(*[pick(back[d], S * r + run) for d in range(N)])).astype(BF)
        z = gcols(b, places(first[r])).astype(np.float32) + x[r].astype(np.float32)
        q = mx_ref.quantize(z.astype(BF))
        y[r] = mx_ref.matmul(mx_ref.quantize(m[r]), q)
        oa[r], ob[r] = first[r], second[r]
        oc[r], osc[r] = emit(q)
    return {"y": y, "oa": oa, "ob": ob, "oc": oc, "osc": osc}

@@ -1,0 +1,718 @@
+import numpy as np
+from concourse.bass import DstId, RemoteDMATransfer
+from concourse.mybir import dt, AluOpType, ActivationFunctionType
+
+C = 512
+RUN = 64
+PC = 128
+NS = 7
+X4, U8 = "float8_e4m3fn_x4", "uint8"
+BF, F32, I32, U16 = "bfloat16", "float32", "int32", "uint16"
+
+PLAN = {
+    "stages1": ((0, 1), (2, 3)),
+    "share1": (4, 4, 3, 4),
+    "share2": (4, 4, 4, 4),
+    "late1": ((4, 0), (4, 0)),
+    "late2": ((3, 2), (2, 1), (4, 0)),
+    "evac": ((2, 3), (2, 3), (), ()),
+    "copy1": "svv",
+    "copy2": "ssvv",
+    "chunks1": ((16, 3),),
+    "chunk2": 1,
+    "tail": 2,
+    "help1": True,
+    "help2": True,
+    "send1": (0, 3, 1, 2),
+    "send2": (2, 3, 1, 0),
+    "home": (1, 2, 3, 0),
+    "out": (128, 384),
+}
+
+
+def _scratch():
+    s = {}
+    def sb(n, w, d):
+        s[n] = ("sbuf", [128, w], d)
+    for n in ("xs", "xp", "ft", "ht", "hp", "hs", "sc", "tt", "zs", "zt", "et"):
+        sb(n, 4 * C, BF)
+    for n in ("us", "vs", "ms", "ones", "half", "jsrc"):
+        sb(n, 512, BF)
+    for n, w in (("qx", C), ("qu", PC), ("ub", PC), ("qv", PC), ("vb", PC), ("qm", PC), ("qe", C), ("wq", C),
+                 ("qf", C), ("aa", C), ("ae", 192), ("ao", 192), ("qh", C), ("qt", C), ("bb", C), ("be", 192),
+                 ("bo", 192), ("qz", C), ("h1", RUN), ("h2", PC)):
+        sb(n + "c", w, X4)
+        sb(n + "s", w, U8)
+    for n in ("1", "2"):
+        sb("r" + n, C, F32)
+        sb("sb" + n, C, F32)
+        sb("eqs" + n, C, BF)
+        sb("sa" + n, 32 * NS, F32)
+        sb("sx" + n, 32 * NS, F32)
+        sb("sob" + n, 32 * 256, BF)
+        sb("w" + n, 544, BF)
+        sb("tr" + n, 1024, BF)
+        sb("sel" + n, 64, F32)
+        sb("pos" + n, 32, U16)
+        sb("plc" + n, 32, U16)
+        sb("ord" + n, 32, U16)
+        sb("out" + n, 528, F32)
+    sb("soa", 32 * 256, BF)
+    sb("msk", 256, F32)
+    sb("eq", 256, BF)
+    sb("mv", 4 * 512, BF)
+    sb("mt", 4 * 512, BF)
+    sb("ia", 256, I32)
+    sb("ib", 256, I32)
+    sb("pick", 256, BF)
+    sb("keep", 256, BF)
+    sb("keepn", 32 * NS, F32)
+    sb("ksel", 64, F32)
+    sb("iu", 8, I32)
+    sb("offu", 8, U16)
+    sb("ip", 8, I32)
+    sb("iq", 8, I32)
+    sb("cols", 8, F32)
+    sb("ys", C, F32)
+    s["ps"] = ("psum", [128, 8 * 512], F32)
+    return s
+
+
+SCRATCH = _scratch()
+SEMAPHORES = (["sv", "ss", "sp", "sg", "ldu", "ldx0", "ldx1", "ldx2", "ldx3", "ldr", "ls", "st", "h1c", "h1s", "h2c", "h2s"]
+              + ["a%d_%d" % (e, k) for e in (1, 2) for k in range(4)])
+
+A = AluOpType
+ACT = ActivationFunctionType
+
+
+def _bits(engines):
+    m = 0
+    for e in engines:
+        m |= 1 << e
+    return m
+
+
+def _helpers(T, topo, home):
+    ok = [c for c in topo.cores_of(home)
+          if T.rank_of(c) is None and all(topo.may_write(c, d) for d in T.cores if d != c)]
+    ok.sort(key=lambda c: (topo.die(c) == topo.die(home), c))
+    return ok[:2]
+
+
+def _view(T, name, a, b):
+    v = T[name][:, a:b]
+    return v.bitcast(dt.uint8) if name.endswith("c") else v
+
+
+def _send(g, T, topo, moves, local):
+    if len(moves) == 1:
+        d, eng, sem, src, dst = moves[0]
+        rid, pid, se = topo.addr(d)
+        g.remote_dma(dst, src, sem, local, pid, rid, _bits(eng))
+    else:
+        tr = []
+        for d, eng, sem, src, dst in moves:
+            rid, pid, se = topo.addr(d)
+            tr.append(RemoteDMATransfer(dst_ids=[DstId(rid=rid, pnc=pid)], dma_engine_mask=_bits(eng),
+                                        remote_sem=sem, src=src, dst=dst))
+        g.remote_dma_fused(tr, local_sem=local)
+    return sum(len(m[1]) for m in moves)
+
+
+def _helper_program(g, core, T, topo):
+    home = [c for c in T.cores if topo.chip(c) == topo.chip(core)]
+    if not home:
+        return
+    hs = _helpers(T, topo, home[0])
+    if core not in hs:
+        return
+    i = hs.index(core)
+    r = T.rank_of(home[0])
+    far = topo.engines(core, T.cores[r ^ 2])
+    near = [e for e in topo.engines(home[0], core) if e not in far]
+    total = 0
+    if PLAN["help1"]:
+        d = 2 * ((r // 2) ^ 3) + i
+        for p in "cs":
+            g.wait_ge(T.sem["h1" + p], len(near) // 2)
+            total += _send(g, T, topo, [(T.cores[d], far, T.sem.a1_3, _view(T, "h1" + p, 0, RUN),
+                                         _view(T, "aa" + p, RUN * r, RUN * r + RUN))], T.sem.ls)
+    if PLAN["help2"]:
+        k = 2 + i
+        a = (r // 2) ^ k
+        h = len(far) // 2
+        for p in "cs":
+            g.wait_ge(T.sem["h2" + p], len(topo.engines(home[0], core)))
+            total += _send(g, T, topo, [(T.cores[2 * a + j], far[h * j:h * j + h], T.sem["a2_%d" % k],
+                                         _view(T, "h2" + p, RUN * j, RUN * j + RUN),
+                                         _view(T, "bb" + p, RUN * r, RUN * r + RUN)) for j in range(2)], T.sem.ls)
+    if total:
+        g.wait_ge(T.sem.ls, total)
+
+
+def rank_program(g, core, T, topo):
+    rank = T.rank_of(core)
+    if rank is None:
+        _helper_program(g, core, T, topo)
+        return
+    a0, odd = rank // 2, rank % 2
+    help1, help2 = PLAN["help1"], PLAN["help2"]
+    queue = {"v": g.vector, "s": g.scalar, "p": g.tensor, "g": g, "y": g.sync}
+    qsem = {"v": "sv", "s": "ss", "p": "sp", "g": "sg"}
+    count = {"sv": 0, "ss": 0, "sp": 0, "sg": 0, "ls": 0, "st": 0}
+    waited = {q: {} for q in queue}
+    tokens = [None]
+    wr, rd = {}, {}
+    for n, (where, shape, dty) in SCRATCH.items():
+        w = 8 if where == "psum" else shape[1]
+        wr[n] = np.zeros(w, np.int64)
+        rd[n] = {q: np.zeros(w, np.int64) for q in qsem}
+
+    def key(n, a, b, s=1):
+        if n == "ps":
+            return (n, slice(a // 512, (b - 1) // 512 + 1))
+        return (n, slice(a, b, s))
+
+    def ap(k):
+        return T[k[0]][:, k[1]:k[2]:k[3]] if len(k) == 4 else T[k[0]][:, k[1]:k[2]]
+
+    def wait(q, sem, val):
+        if waited[q].get(sem, 0) < val:
+            queue[q].wait_ge(T.sem[sem], int(val))
+            waited[q][sem] = int(val)
+
+    def need(q, reads, writes=()):
+        want = {}
+        def add(sem, val):
+            if val > want.get(sem, 0):
+                want[sem] = int(val)
+        for k in list(reads) + list(writes):
+            n, sl = key(*k)
+            for t in np.unique(wr[n][sl]):
+                if t:
+                    add(*tokens[int(t)])
+        for k in reads:
+            if k[0] == "ps":
+                n, sl = key(*k)
+                for o in qsem:
+                    if o != q:
+                        add(qsem[o], rd[n][o][sl].max())
+        for k in writes:
+            n, sl = key(*k)
+            for o in qsem:
+                add(qsem[o], rd[n][o][sl].max())
+        for sem, val in want.items():
+            wait(q, sem, val)
+
+    def wrote(keys, sem, val):
+        tokens.append((sem, val))
+        for k in keys:
+            n, sl = key(*k)
+            wr[n][sl] = len(tokens) - 1
+
+    def op(q, make, reads, writes):
+        need(q, reads, writes)
+        sem = qsem[q]
+        make().then_inc(T.sem[sem], 1)
+        count[sem] += 1
+        for k in reads:
+            n, sl = key(*k)
+            rd[n][q][sl] = count[sem]
+        wrote(writes, sem, count[sem])
+
+    V, S, P = g.vector, g.scalar, g.tensor
+
+    def aps(*ks):
+        return [k for k in ks if isinstance(k, tuple)]
+
+    def val(k):
+        return ap(k) if isinstance(k, tuple) else k
+
+    def memset(o, c):
+        op("v", lambda: V.memset(ap(o), c), [], [o])
+
+    def ts(o, i, s1, s2, o0, o1=None):
+        if o1 is None:
+            op("v", lambda: V.tensor_scalar(ap(o), ap(i), val(s1), None, o0), aps(i, s1), [o])
+        else:
+            op("v", lambda: V.tensor_scalar(ap(o), ap(i), val(s1), val(s2), o0, o1), aps(i, s1, s2), [o])
+
+    def tt(o, i0, i1, o0):
+        op("v", lambda: V.tensor_tensor(ap(o), ap(i0), ap(i1), o0), [i0, i1], [o])
+
+    def scan(o, d0, d1, init, o0, o1):
+        op("v", lambda: V.tensor_tensor_scan(ap(o), ap(d0), ap(d1), val(init), o0, o1), aps(d0, d1, init), [o])
+
+    def act(o, i, func, bias=None, scale=None, acc=None):
+        kw = {}
+        if bias is not None:
+            kw["bias"] = val(bias)
+        if scale is not None:
+            kw["scale"] = scale
+        if acc is not None:
+            kw["accum_out"] = ap(acc)
+        op("s", lambda: S.activation(ap(o), ap(i), func, **kw), aps(i, bias), aps(o, acc))
+
+    def copy(o, i, q="v"):
+        if q == "v":
+            op("v", lambda: V.tensor_copy(ap(o), ap(i)), [i], [o])
+        else:
+            act(o, i, ACT.Copy)
+
+    def gather(q, o, win, off):
+        if q == "v":
+            op("v", lambda: V.tensor_copy(ap(o), ap(win).indirect(ap(off))), [win, off], [o])
+        else:
+            op("s", lambda: S.activation(ap(o), ap(win).indirect(ap(off)), ACT.Copy), [win, off], [o])
+
+    def quant(name, c0, n, src, s0):
+        oc, os_, i = (name + "c", c0, c0 + n), (name + "s", c0, c0 + n), (src, 4 * s0, 4 * (s0 + n))
+        op("v", lambda: V.quantize_mx(ap(oc), ap(os_), ap(i)), [i], [oc, os_])
+
+    def mm(bank, w, w0, x, x0, n):
+        ks = [(w + "c", w0, w0 + PC), (w + "s", w0, w0 + PC), (x + "c", x0, x0 + n), (x + "s", x0, x0 + n)]
+        o = ("ps", 512 * bank, 512 * bank + n)
+        op("p", lambda: P.matmul_mx(ap(o), ap(ks[0]), ap(ks[1]), ap(ks[2]), ap(ks[3]), True, True), ks, [o])
+
+    def iota(o, pattern, base, cm, loose=False):
+        if loose:
+            op("g", lambda: g.iota(ap(o), pattern, base, cm, allow_small_or_imprecise_dtypes=True), [], [o])
+        else:
+            op("g", lambda: g.iota(ap(o), pattern, base, cm), [], [o])
+
+    def planes(dst, src, c0, n):
+        for b in range(4):
+            o, i = (dst, C * b + c0, C * b + c0 + n), (src, 4 * c0 + b, 4 * (c0 + n), 4)
+            op("g", lambda: g.affine_select(ap(o), ap(i), [[0, n]], A.is_ge, 0.0, 0, 0), [i], [o])
+
+    def store(q, out, src, reads):
+        need(q, reads)
+        queue[q].dma_start(out, src).then_inc(T.sem.st, 16)
+        count["st"] += 16
+
+    def spread(n):
+        qc, qs, bc, bs, off = ("q" + n + "c", 0, PC), ("q" + n + "s", 0, PC), (n + "bc", 0, PC), (n + "bs", 0, PC), ("offu", 0, 8)
+        quant("q" + n, 0, PC, n + "s", 0)
+        op("v", lambda: V.tensor_copy(ap(bc).bitcast(dt.uint32), ap(qc).bitcast(dt.uint32).indirect(ap(off))), [qc, off], [bc])
+        gather("s", bs, qs, off)
+
+    g.sync.dma_start(T.us[:], T.u[:]).then_inc(T.sem.ldu, 16)
+    wrote([("us", 0, 512)], "ldu", 16)
+    count["ldu"] = 16
+    for i, pcs in enumerate(PLAN["stages1"]):
+        lo, hi = 4 * PC * pcs[0], 4 * PC * (pcs[-1] + 1)
+        g.sync.dma_start(T.xs[:, lo:hi], T.x[:, lo:hi]).then_inc(T.sem["ldx%d" % i], 16)
+        wrote([("xs", lo, hi)], "ldx%d" % i, 16)
+        count["ldx%d" % i] = 16
+    wait("y", "ldx%d" % (len(PLAN["stages1"]) - 1), 16)
+    g.sync.dma_start(T.vs[:], T.v[:]).then_inc(T.sem.ldr, 16)
+    g.sync.dma_start(T.ms[:], T.m[:]).then_inc(T.sem.ldr, 16)
+    g.sync.dma_start(T.wqc[:].bitcast(dt.uint8), T.wc[:]).then_inc(T.sem.ldr, 16)
+    g.sync.dma_start(T.wqs[:], T.ws[:]).then_inc(T.sem.ldr, 16)
+    wrote([("vs", 0, 512), ("ms", 0, 512), ("wqc", 0, C), ("wqs", 0, C)], "ldr", 64)
+    count["ldr"] = 64
+
+    hs = _helpers(T, topo, core)
+    far = topo.engines(core, T.cores[rank ^ 1])
+    both = topo.engines(core, hs[0])
+    near = [e for e in both if e not in far]
+    for e, land, pair in ((1, "aa", "a"), (2, "bb", "b")):
+        for k in range(4):
+            n = 2 * len(far) * (2 if (e == 1 and k == 3 and help1) else 1)
+            count["a%d_%d" % (e, k)] = n
+            if k:
+                name, c0, w = land, PC * (a0 ^ k), PC
+            else:
+                name, c0, w = pair + "eo"[odd], 128 * odd, RUN
+            wrote([(name + "c", c0, c0 + w), (name + "s", c0, c0 + w)], "a%d_%d" % (e, k), n)
+
+    def pack(e, k, tile):
+        if k:
+            quant("qf" if e == 1 else "qt", PC * (a0 ^ k), PC, tile, PC * (a0 ^ k))
+        else:
+            quant("ab"[e - 1] + "eo"[odd], RUN * (1 - odd), PC, tile, PC * a0)
+
+    def send(e, k):
+        src, land, pair = ("qf", "aa", "a") if e == 1 else ("qt", "bb", "b")
+        sem = T.sem["a%d_%d" % (e, k)]
+        a = a0 ^ k
+        for p in "cs":
+            if k == 0:
+                c0 = 128 * (1 - odd)
+                need("g", [(pair + "eo"[odd] + p, c0, c0 + RUN)])
+                mv = [(T.cores[rank ^ 1], far, sem, _view(T, pair + "eo"[odd] + p, c0, c0 + RUN),
+                       _view(T, pair + "oe"[odd] + p, c0, c0 + RUN))]
+            else:
+                need("g", [(src + p, PC * a, PC * a + PC)])
+                if e == 1 and k == 3 and help1:
+                    h = len(near) // 2
+                    mv = [(hs[j], near[h * j:h * j + h], T.sem["h1" + p],
+                           _view(T, src + p, PC * a + RUN * j, PC * a + RUN * j + RUN), _view(T, "h1" + p, 0, RUN))
+                          for j in range(2)]
+                elif e == 2 and k >= 2 and help2:
+                    mv = [(hs[k - 2], both, T.sem["h2" + p], _view(T, src + p, PC * a, PC * a + PC),
+                           _view(T, "h2" + p, 0, PC))]
+                else:
+                    h = len(far) // 2
+                    mv = [(T.cores[2 * a + j], far[h * j:h * j + h], sem,
+                           _view(T, src + p, PC * a + RUN * j, PC * a + RUN * j + RUN),
+                           _view(T, land + p, RUN * rank, RUN * rank + RUN)) for j in range(2)]
+            count["ls"] += _send(g, T, topo, mv, T.sem.ls)
+
+    def arrived(e, k):
+        if k:
+            c0 = PC * (a0 ^ k)
+            return ("aa" if e == 1 else "bb"), c0, [(0, c0, PC)]
+        c0 = PC * a0
+        return "ab"[e - 1] + "eo"[odd], RUN * odd, [(0, c0 + RUN, RUN), (RUN, c0, RUN)]
+
+    H16, TWO, NEG, ADD, KOD = [("cols", i, i + 1) for i in range(5)]
+    iota(("iu", 0, 8), [[16, 8]], 0, 0)
+    iota(("ia", 0, 256), [[1, 256]], 128, -1)
+    iota(("ip", 0, 8), [[0, 8]], 0, 1)
+    iota(("jsrc", 0, 512), [[1, 512]], -256, 0, True)
+    memset(("sa1", 0, 32 * NS), 0.0)
+    memset(("sob1", 255, 32 * 256, 256), 0.0)
+    copy(("offu", 0, 8), ("iu", 0, 8))
+    memset(("w1", 0, 544), 0.0)
+    memset(("ones", 0, 512), 1.0)
+    ts(("ib", 0, 256), ("ia", 0, 256), 15, None, A.bitwise_and)
+    memset(("keepn", 0, 32 * NS), 1.0)
+    ts(("iq", 0, 8), ("ip", 0, 8), 16, None, A.bitwise_and)
+    ts(("pick", 0, 256), ("ib", 0, 256), 0.0, None, A.is_equal)
+    copy(H16, ("iq", 0, 1))
+    ts(("keep", 0, 256), ("ib", 0, 256), 0.0, None, A.not_equal)
+    memset(("keepn", 0, 32 * NS, NS), 0.0)
+    memset(("ksel", 0, 64), -4096.0)
+    ts(TWO, H16, 2.0, 512.0, A.mult, A.add)
+    ts(NEG, H16, -1.0, None, A.mult)
+    ts(ADD, H16, 64.0, -768.0, A.mult, A.add)
+    ts(KOD, H16, -320.0, 1024.0, A.mult, A.add)
+    ts(("ksel", 1, 64, 2), ("ksel", 0, 64, 2), 0.0, KOD, A.mult, A.add)
+    spread("u")
+
+    def sorter(n, nstage):
+        st = {"pv": None, "ps": None, "nv": 0, "ns": 0, "last": {}, "slot": {}, "have": [], "dv": [], "ds": [], "stage": 0,
+              "scalar": set(), "done": set(), "fin": set(), "tail": []}
+        r, sbn, sa, sx, w = "r" + n, "sb" + n, "sa" + n, "sx" + n, "w" + n
+
+        def own(m):
+            return (sbn, 16 * m + 15, 16 * m + 16)
+
+        def segments(m, pieces):
+            runs = []
+            for a in sorted(pieces):
+                if runs and runs[-1][1] == PC * a:
+                    runs[-1][1] += PC
+                else:
+                    runs.append([PC * a, PC * a + PC])
+            cut = 16 * m + 16
+            ge = [(lo, min(hi, cut), True) for lo, hi in runs if lo < cut]
+            gt = [(max(lo, cut), hi, False) for lo, hi in runs if hi > cut]
+            return runs, ge + gt
+
+        def flush(which):
+            if st[which]:
+                st[which]()
+                st[which] = None
+
+        def task_v(t):
+            m, pieces, stage = t
+            base = 512 * (st["nv"] % 4)
+            st["nv"] += 1
+            at = base
+            for lo, hi, tie in segments(m, pieces)[1]:
+                ts(("mv", at, at + hi - lo), (r, lo, hi), own(m), 0.5, A.is_ge if tie else A.is_gt, A.subtract)
+                at += hi - lo
+            flush("pv")
+            h = (at - base) // 2
+            so = ("sob" + n) if (nstage - 1 - stage) % 2 == 0 else "soa"
+            end = 256 * m + 256
+            def later():
+                scan((so, end - h, end), ("mv", base, base + h), ("mv", base + h, base + 2 * h),
+                     st["last"].get(m, 0.0), A.add, A.add)
+                st["last"][m] = (so, end - 1, end)
+                if stage == nstage - 1:
+                    st["fin"].add(m)
+            st["pv"] = later
+
+        def task_s(t):
+            m, pieces, stage = t
+            base = 512 * (st["ns"] % 4)
+            st["ns"] += 1
+            runs, segs = segments(m, pieces)
+            at = base
+            for lo, hi in runs:
+                act(("mt", at, at + hi - lo), (r, lo, hi), ACT.Sign, bias=own(m), scale=-1.0)
+                at += hi - lo
+            flush("ps")
+            mid = base + sum(hi - lo for lo, hi, tie in segs if tie)
+            def later():
+                for lo, hi, bias in ((base, mid, 0.5), (mid, at, -0.5)):
+                    if hi > lo:
+                        sl = st["slot"].get(m, 2)
+                        st["slot"][m] = sl + 1
+                        act(("mt", lo, hi), ("mt", lo, hi), ACT.Sign, bias=bias, scale=-1.0,
+                            acc=(sa, NS * m + sl, NS * m + sl + 1))
+            st["ps"] = later
+
+        def fill_v(k):
+            for t in st["dv"][:k]:
+                task_v(t)
+            st["dv"] = st["dv"][k:]
+
+        def chunk(ms):
+            ms = sorted(set(ms) - st["done"])
+            st["done"] |= set(ms)
+            runs = []
+            for m in ms:
+                if runs and runs[-1][1] == m:
+                    runs[-1][1] = m + 1
+                else:
+                    runs.append([m, m + 1])
+            win = (w, 0, 528)
+            def one():
+                assert all(m in st["scalar"] or m in st["fin"] for m in ms)
+                for lo, hi in runs:
+                    if not all(m in st["scalar"] for m in range(lo, hi)):
+                        ts((sa, NS * lo + 1, NS * hi, NS), ("sob" + n, 256 * lo + 255, 256 * hi, 256), 2.0, None, A.mult)
+            def two():
+                for lo, hi in runs:
+                    scan((sx, NS * lo, NS * hi), ("keepn", 0, NS * (hi - lo)), (sa, NS * lo, NS * hi), 0.0, A.mult, A.add)
+            def three():
+                for lo, hi in runs:
+                    ts(("pos" + n, lo, hi), (sx, NS * lo + NS - 1, NS * hi, NS), 0.5, None, A.mult)
+            def four():
+                for lo, hi in runs:
+                    off, src = ("pos" + n, lo, hi), ("jsrc", 16 * lo, 16 * hi)
+                    op("v", lambda: V.tensor_copy(ap(win).indirect(ap(off)), ap(src)), [off, src], [win])
+            return [one, two, three, four]
+
+        def stage(pieces, shares, wside, x, late, copier, chunks=()):
+            s = st["stage"]
+            st["stage"] += 1
+            c0, wd = PC * min(pieces), PC * len(pieces)
+            bv, bs = 4 + s % 2, (6 if copier == "s" else 4) + s % 2
+            mm(bv, wside, 0, x, c0, wd)
+            if bs != bv:
+                mm(bs, wside, 0, x, c0, wd)
+            fill_v(99)
+            for t in st["ds"]:
+                task_s(t)
+            st["ds"] = []
+            copy((r, c0, c0 + wd), ("ps", 512 * bs, 512 * bs + wd), copier)
+            pv = ("ps", 512 * bv, 512 * bv + wd)
+            extras = [lambda: tt(("msk", 0, wd), pv, ("pick", 0, wd), A.mult),
+                      lambda: scan((sbn, c0, c0 + wd), ("keep", 0, wd), ("msk", 0, wd), 0.0, A.mult, A.add),
+                      lambda: tt(("eq", 0, wd), pv, (sbn, c0, c0 + wd), A.is_equal),
+                      lambda: scan(("eqs" + n, c0, c0 + wd), ("keep", 0, wd), ("eq", 0, wd), 0.0, A.mult, A.add)]
+            if s == nstage - 1:
+                extras.append(lambda: ts((sa, 0, 32 * NS, NS), ("eqs" + n, 15, C, 16), -2.0, TWO, A.mult, A.add))
+            old = [m for a in st["have"] for m in range(8 * a, 8 * a + 8)]
+            st["have"] = st["have"] + list(pieces)
+            new = []
+            for a, k in zip(pieces, shares):
+                new += list(range(8 * a, 8 * a + 8))
+                st["scalar"] |= set(range(8 * a + 8 - k, 8 * a + 8))
+            k = min(shares[-1], PLAN["tail"]) // 2 * 2
+            st["tail"] = list(range(8 * pieces[-1] + 8 - k, 8 * pieces[-1] + 8))
+            tasks = [(m, list(pieces), s) for m in old] + [(m, list(st["have"]), s) for m in new]
+            tv = [t for t in tasks if t[0] not in st["scalar"]]
+            tsc = [t for t in tasks if t[0] in st["scalar"]]
+            kv, ks = late
+            tv, st["dv"] = tv[:len(tv) - kv], tv[len(tv) - kv:]
+            tsc, st["ds"] = tsc[:len(tsc) - ks], tsc[len(tsc) - ks:]
+            if not old:
+                extras.pop(0)()
+                extras.pop(0)()
+            head = min(len(extras), len(tv))
+            for t in tv[:head]:
+                extras.pop(0)()
+                task_v(t)
+            for x_ in extras:
+                x_()
+            for t in tsc:
+                task_s(t)
+            if s == nstage - 1:
+                flush("ps")
+            steps = []
+            rest = tv[head:]
+            for i, t in enumerate(rest):
+                task_v(t)
+                for ms, before in chunks:
+                    if len(rest) - 1 - i == before:
+                        steps += chunk(ms)
+                for f in steps[:2]:
+                    f()
+                steps = steps[2:]
+            if s == nstage - 1:
+                flush("pv")
+            for f in steps:
+                f()
+
+        def finish():
+            for f in chunk([m for m in range(32) if m not in st["tail"]]) + chunk(st["tail"]):
+                f()
+            tr, sel = "tr" + n, "sel" + n
+            ts(("plc" + n, 0, 32), (sx, NS - 1, 32 * NS, NS), 0.5, NEG, A.mult, A.add)
+            for par in range(2):
+                o, i = (tr, 512 * par, 512 * par + 512), (w, 16 * par, 16 * par + 512)
+                op("v", lambda: V.transpose(ap(o), ap(i)), [i], [o])
+            scan((sel, 0, 64), ("ksel", 0, 64), (tr, 0, 1024, 16), 0.0, A.add, A.max)
+            for par in range(2):
+                ts(("ord" + n, par, 32, 2), (sel, 32 * par + 1, 32 * par + 32, 2), ADD, None, A.add)
+
+        def emit(out):
+            act(("out" + n, 0, 528), (w, 0, 528), ACT.Identity, bias=256.0)
+            for gr in range(8):
+                o = 16 * (gr % 2)
+                store("y", out[gr:gr + 1, :], T["out" + n][16 * gr:16 * gr + 1, o:o + C], [("out" + n, 0, 528)])
+
+        return stage, fill_v, finish, emit
+
+    last = len(PLAN["stages1"]) - 1
+    stage, fill_v, finish, emit = sorter("1", last + 1)
+    for i, pcs in enumerate(PLAN["stages1"]):
+        quant("qx", PC * pcs[0], PC * len(pcs), "xs", PC * pcs[0])
+        stage(list(pcs), [PLAN["share1"][a] for a in pcs], "ub", "qx", PLAN["late1"][i] if i < last else (0, 0),
+              PLAN["copy1"][i], [(range(hi), before) for hi, before in PLAN["chunks1"]] if i == last else ())
+    planes("xp", "xs", 0, C)
+    for b in range(4):
+        o, i = ("et", 512 * b, 512 * b + 512), ("ones", 0, 512)
+        op("g", lambda: g.affine_select(ap(o), ap(i), [[8, 128], [1, 4]], A.is_equal, 0.0, -b, -8), [i], [o])
+    finish()
+
+    def move(q, tile, win, lst, c0, n, b):
+        gather(q, (tile, 4 * c0 + b, 4 * (c0 + n), 4), (win, C * b, C * b + C), (lst, c0 // 16, (c0 + n) // 16))
+
+    order1 = PLAN["send1"]
+    mine = ((0, 1), (0, 1), (0,), (0, 1))
+    for i, k in enumerate(order1):
+        for b in range(4):
+            if b not in mine[i]:
+                move("s", "ft", "xp", "ord1", PC * (a0 ^ k), PC, b)
+    for i, k in enumerate(order1):
+        for j, b in enumerate(mine[i]):
+            move("v", "ft", "xp", "ord1", PC * (a0 ^ k), PC, b)
+            if j == 0 and i > 1:
+                pack(1, order1[i - 1], "ft")
+                send(1, order1[i - 1])
+        if i in (0, 3):
+            pack(1, k, "ft")
+            send(1, k)
+    emit(T.oa)
+
+    spread("v")
+    memset(("sa2", 0, 32 * NS), 0.0)
+    memset(("sob2", 255, 32 * 256, 256), 0.0)
+    memset(("w2", 0, 544), 0.0)
+    memset(("half", 0, 512), 0.5)
+    quant("qm", 0, PC, "ms", 0)
+    for b in range(4):
+        quant("qe", PC * b, PC, "et", PC * b)
+
+    stage, fill_v, finish, emit = sorter("2", 4)
+    for k in range(4):
+        x, x0, parts = arrived(1, k)
+        for b in range(4):
+            mm(b, "wq", PC * b, x, x0, PC)
+        for b in (0, 2, 1, 3):
+            for at, c0, wd in parts:
+                o, i = ("ht", 4 * c0 + b, 4 * (c0 + wd), 4), ("ps", 512 * b + at, 512 * b + at + wd)
+                if b in PLAN["evac"][k]:
+                    act(o, i, ACT.Copy, scale=0.00390625)
+                else:
+                    ts(o, i, 0.00390625, None, A.mult)
+        fill_v(1)
+        a = a0 ^ k
+        quant("qh", PC * a, PC, "ht", PC * a)
+        planes("hp", "ht", PC * a, PC)
+        stage([a], [PLAN["share2"][k]], "vb", "qh", PLAN["late2"][k] if k < 3 else (0, 0), PLAN["copy2"][k],
+              [([m for m in range(32) if m // 8 != a], PLAN["chunk2"])] if k == 3 else ())
+    finish()
+
+    def sort_h(q, b, c0, n):
+        gather(q, ("hs", C * b + c0, C * b + c0 + n), ("hp", C * b, C * b + C), ("ord2", c0 // 16, (c0 + n) // 16))
+
+    def run(b):
+        scan(("sc", C * b, C * b + C), ("half", 0, C), ("hs", C * b, C * b + C), 0.0, A.mult, A.max)
+
+    sort_h("s", 1, 0, C)
+    sort_h("s", 2, 0, C)
+    sort_h("s", 3, 256, 256)
+    sort_h("v", 0, 0, C)
+    sort_h("v", 3, 0, 256)
+    for b in range(4):
+        run(b)
+    order2 = PLAN["send2"]
+    mine = ((3,), (3,), (3, 2), (3, 2))
+    for i, k in enumerate(order2):
+        for b in range(4):
+            if b not in mine[i]:
+                move("s", "tt", "sc", "plc2", PC * (a0 ^ k), PC, b)
+    for i, k in enumerate(order2):
+        for j, b in enumerate(mine[i]):
+            move("v", "tt", "sc", "plc2", PC * (a0 ^ k), PC, b)
+            if j == 0 and i > 0:
+                pack(2, order2[i - 1], "tt")
+                send(2, order2[i - 1])
+    pack(2, order2[3], "tt")
+    send(2, order2[3])
+    emit(T.ob)
+
+    comes = [("b" + "eo"[odd], RUN * (1 - odd), [(RUN * odd, PC * a0 + RUN * odd, RUN)])]
+    for k in PLAN["home"]:
+        x, x0, parts = arrived(2, k)
+        comes.append((x, x0, parts if k else [parts[odd]]))
+    for i, (x, x0, parts) in enumerate(comes):
+        for b in range(4):
+            mm(4 * (i % 2) + b, "qe", PC * b, x, x0, PC)
+        for b in range(4):
+            for at, c0, wd in parts:
+                bank = 512 * (4 * (i % 2) + b)
+                tt(("zs", C * b + c0, C * b + c0 + wd), ("ps", bank + at, bank + at + wd),
+                   ("ft", 4 * c0 + b, 4 * (c0 + wd), 4), A.add)
+    cuts = [0]
+    for wd in PLAN["out"]:
+        cuts.append(cuts[-1] + wd)
+    nout = len(PLAN["out"])
+
+    def result(h):
+        lo, hi = cuts[h], cuts[h + 1]
+        if h == nout - 1 and hi - lo >= 2 * PC:
+            mid = (lo + hi) // 2
+            mm(6, "qm", 0, "qz", lo, mid - lo)
+            mm(7, "qm", 0, "qz", mid, hi - mid)
+            copy(("ys", lo, mid), ("ps", 512 * 6, 512 * 6 + mid - lo))
+            copy(("ys", mid, hi), ("ps", 512 * 7, 512 * 7 + hi - mid), "s")
+        else:
+            mm(h, "qm", 0, "qz", lo, hi - lo)
+            copy(("ys", lo, hi), ("ps", 512 * h, 512 * h + hi - lo), "s")
+        store("s" if h == nout - 1 else "y", T.y[:, lo:hi], T.ys[:, lo:hi], [("ys", lo, hi)])
+
+    def close(h):
+        lo, hi = cuts[h], cuts[h + 1]
+        quant("qz", lo, hi - lo, "zt", lo)
+        store("y", T.oc[:, 4 * lo:4 * hi], _view(T, "qzc", lo, hi), [("qzc", lo, hi)])
+
+    for h in range(nout):
+        lo, hi = cuts[h], cuts[h + 1]
+        for b in ((0, 1, 2) if h == 0 else (0, 1)):
+            move("s", "zt", "zs", "plc1", lo, hi - lo, b)
+        if h > 1:
+            result(h - 2)
+        move("v", "zt", "zs", "plc1", lo, hi - lo, 3)
+        if h:
+            close(h - 1)
+            move("v", "zt", "zs", "plc1", lo, hi - lo, 2)
+    if nout > 1:
+        result(nout - 2)
+    close(nout - 1)
+    for k in range(4):
+        store("y", T.osc[4 * k:4 * k + 4, :], T.qzs[32 * k:32 * k + 4, :], [("qzs", 0, C)])
+    result(nout - 1)
+
+    for sem, n in count.items():
+        if n:
+            wait("g", sem, n)

@@ -5,26 +5,23 @@ from concourse.mybir import dt, AluOpType, ActivationFunctionType
 C = 512
 RUN = 64
 PC = 128
-NS = 7
+D = 9
+CW = 30
+BIG = 2.0 ** 90
 X4, U8 = "float8_e4m3fn_x4", "uint8"
 BF, F32, I32, U16 = "bfloat16", "float32", "int32", "uint16"
 
 PLAN = {
-    "stages1": ((0, 1), (2, 3)),
-    "share1": (4, 4, 3, 4),
-    "share2": (4, 4, 4, 4),
-    "late1": ((4, 0), (4, 0)),
-    "late2": ((3, 2), (2, 1), (4, 0)),
-    "evac": ((2, 3), (2, 3), (), ()),
-    "copy1": "svv",
-    "copy2": "ssvv",
-    "chunks1": ((16, 3),),
-    "chunk2": 1,
-    "tail": 2,
-    "help1": True,
-    "help2": True,
-    "send1": (0, 3, 1, 2),
-    "send2": (2, 3, 1, 0),
+    "vlong": (7, 7),
+    "sr": (6, 6),
+    "early": ((2, 4), (3, 3)),
+    "between": ((2, 5), (1, 0)),
+    "psum": (False, False),
+    "proc": (0, 1, 2, 3),
+    "evac": ((2, 3), (2, 3), (2, 3), (2, 3)),
+    "route": ("dds", "d01"),
+    "wide": (False, True),
+    "send": ((0, 1, 3, 2), (2, 3, 1, 0)),
     "home": (1, 2, 3, 0),
     "out": (128, 384),
 }
@@ -40,47 +37,29 @@ def _scratch():
         sb(n, 512, BF)
     for n, w in (("qx", C), ("qu", PC), ("ub", PC), ("qv", PC), ("vb", PC), ("qm", PC), ("qe", C), ("wq", C),
                  ("qf", C), ("aa", C), ("ae", 192), ("ao", 192), ("qh", C), ("qt", C), ("bb", C), ("be", 192),
-                 ("bo", 192), ("qz", C), ("h1", RUN), ("h2", PC)):
+                 ("bo", 192), ("qz", C), ("h1", C), ("h2", C)):
         sb(n + "c", w, X4)
         sb(n + "s", w, U8)
     for n in ("1", "2"):
-        sb("r" + n, C, F32)
-        sb("sb" + n, C, F32)
-        sb("eqs" + n, C, BF)
-        sb("sa" + n, 32 * NS, F32)
-        sb("sx" + n, 32 * NS, F32)
-        sb("sob" + n, 32 * 256, BF)
-        sb("w" + n, 544, BF)
-        sb("tr" + n, 1024, BF)
-        sb("sel" + n, 64, F32)
-        sb("pos" + n, 32, U16)
-        sb("plc" + n, 32, U16)
-        sb("ord" + n, 32, U16)
-        sb("out" + n, 528, F32)
-    sb("soa", 32 * 256, BF)
-    sb("msk", 256, F32)
-    sb("eq", 256, BF)
-    sb("mv", 4 * 512, BF)
-    sb("mt", 4 * 512, BF)
-    sb("ia", 256, I32)
-    sb("ib", 256, I32)
-    sb("pick", 256, BF)
-    sb("keep", 256, BF)
-    sb("keepn", 32 * NS, F32)
-    sb("ksel", 64, F32)
-    sb("iu", 8, I32)
-    sb("offu", 8, U16)
-    sb("ip", 8, I32)
-    sb("iq", 8, I32)
-    sb("cols", 8, F32)
-    sb("ys", C, F32)
+        for k, w, d in (("r", C, F32), ("sb", C, F32), ("gs", C, BF), ("ra", 64, F32), ("rv", 32 * 256, BF), ("rc", 68, F32),
+                        ("ea", 32, F32), ("eb", 32, F32), ("ec", 32, F32), ("w", 544, BF), ("tr", 1024, BF),
+                        ("sel", 64, F32), ("pos", 32, U16), ("plc", 32, U16), ("ord", 32, U16), ("out", 528, F32)):
+            sb(k + n, w, d)
+    for k, w, d in (("ma", D * C, BF), ("mb", D * C, BF), ("cum", 16 + D * C, BF), ("cs", 544, BF), ("ta", 512, BF),
+                    ("tb", 544, BF), ("xa", 512, BF), ("xb", 544, BF), ("mk", 544, BF), ("mi", 544, BF),
+                    ("msk", 256, F32), ("mt", 4 * 256, BF), ("ia", 256, I32), ("ib", 256, I32), ("pick", 256, BF),
+                    ("cm", 256, BF), ("rst", 256, BF), ("keep", 256, BF), ("kc", 32, F32), ("ksel", 64, F32),
+                    ("iu", 8, I32), ("offu", 8, U16), ("ip", 8, I32), ("iq", 8, I32), ("ir", 8, I32), ("cols", 8, F32),
+                    ("ys", C, F32)):
+        sb(k, w, d)
     s["ps"] = ("psum", [128, 8 * 512], F32)
     return s
 
 
 SCRATCH = _scratch()
-SEMAPHORES = (["sv", "ss", "sp", "sg", "ldu", "ldx0", "ldx1", "ldx2", "ldx3", "ldr", "ls", "st", "h1c", "h1s", "h2c", "h2s"]
-              + ["a%d_%d" % (e, k) for e in (1, 2) for k in range(4)])
+SEMAPHORES = (["sv", "ss", "sp", "sg", "ldu", "ldx0", "ldx1", "ldr", "ls", "st"]
+              + ["a%d_%d" % (e, k) for e in (1, 2) for k in range(4)]
+              + ["h%d%d%s" % (e, k, p) for e in (1, 2) for k in range(1, 4) for p in "cs"])
 
 A = AluOpType
 ACT = ActivationFunctionType
@@ -97,7 +76,7 @@ def _helpers(T, topo, home):
     ok = [c for c in topo.cores_of(home)
           if T.rank_of(c) is None and all(topo.may_write(c, d) for d in T.cores if d != c)]
     ok.sort(key=lambda c: (topo.die(c) == topo.die(home), c))
-    return ok[:2]
+    return ok[:3]
 
 
 def _view(T, name, a, b):
@@ -120,6 +99,13 @@ def _send(g, T, topo, moves, local):
     return sum(len(m[1]) for m in moves)
 
 
+def _engines(T, topo, home, e):
+    far = topo.engines(home, T.cores[T.rank_of(home) ^ 1])
+    both = topo.engines(home, _helpers(T, topo, home)[0])
+    near = [x for x in both if x not in far]
+    return far, near, (both if PLAN["wide"][e - 1] else near)
+
+
 def _helper_program(g, core, T, topo):
     home = [c for c in T.cores if topo.chip(c) == topo.chip(core)]
     if not home:
@@ -130,23 +116,22 @@ def _helper_program(g, core, T, topo):
     i = hs.index(core)
     r = T.rank_of(home[0])
     far = topo.engines(core, T.cores[r ^ 2])
-    near = [e for e in topo.engines(home[0], core) if e not in far]
     total = 0
-    if PLAN["help1"]:
-        d = 2 * ((r // 2) ^ 3) + i
-        for p in "cs":
-            g.wait_ge(T.sem["h1" + p], len(near) // 2)
-            total += _send(g, T, topo, [(T.cores[d], far, T.sem.a1_3, _view(T, "h1" + p, 0, RUN),
-                                         _view(T, "aa" + p, RUN * r, RUN * r + RUN))], T.sem.ls)
-    if PLAN["help2"]:
-        k = 2 + i
-        a = (r // 2) ^ k
-        h = len(far) // 2
-        for p in "cs":
-            g.wait_ge(T.sem["h2" + p], len(topo.engines(home[0], core)))
-            total += _send(g, T, topo, [(T.cores[2 * a + j], far[h * j:h * j + h], T.sem["a2_%d" % k],
-                                         _view(T, "h2" + p, RUN * j, RUN * j + RUN),
-                                         _view(T, "bb" + p, RUN * r, RUN * r + RUN)) for j in range(2)], T.sem.ls)
+    for e in (1, 2):
+        near, wide = _engines(T, topo, home[0], e)[1:]
+        for k in PLAN["send"][e - 1]:
+            how = PLAN["route"][e - 1][k - 1] if k else "d"
+            js = {"s": [[0], [1], []][i], "n": [[], [], [1]][i], str(i): [0, 1]}.get(how)
+            if not js:
+                continue
+            a = (r // 2) ^ k
+            h = len(far) // len(js)
+            for p in "cs":
+                g.wait_ge(T.sem["h%d%d%s" % (e, k, p)], {"s": len(wide) // 2, "n": len(near)}.get(how, len(wide)))
+                total += _send(g, T, topo, [(T.cores[2 * a + j], far[h * n:h * n + h], T.sem["a%d_%d" % (e, k)],
+                                             _view(T, "h%d%s" % (e, p), PC * k + RUN * j, PC * k + RUN * j + RUN),
+                                             _view(T, ("aa", "bb")[e - 1] + p, RUN * r, RUN * r + RUN))
+                                            for n, j in enumerate(js)], T.sem.ls)
     if total:
         g.wait_ge(T.sem.ls, total)
 
@@ -157,7 +142,9 @@ def rank_program(g, core, T, topo):
         _helper_program(g, core, T, topo)
         return
     a0, odd = rank // 2, rank % 2
-    help1, help2 = PLAN["help1"], PLAN["help2"]
+    pieces = [a0 ^ k for k in PLAN["proc"]]
+    up = a0 // 2
+    sg = 1.0 if up else -1.0
     queue = {"v": g.vector, "s": g.scalar, "p": g.tensor, "g": g, "y": g.sync}
     qsem = {"v": "sv", "s": "ss", "p": "sp", "g": "sg"}
     count = {"sv": 0, "ss": 0, "sp": 0, "sg": 0, "ls": 0, "st": 0}
@@ -244,6 +231,9 @@ def rank_program(g, core, T, topo):
     def scan(o, d0, d1, init, o0, o1):
         op("v", lambda: V.tensor_tensor_scan(ap(o), ap(d0), ap(d1), val(init), o0, o1), aps(d0, d1, init), [o])
 
+    def turn(o, i):
+        op("v", lambda: V.transpose(ap(o), ap(i)), [i], [o])
+
     def act(o, i, func, bias=None, scale=None, acc=None):
         kw = {}
         if bias is not None:
@@ -281,6 +271,9 @@ def rank_program(g, core, T, topo):
         else:
             op("g", lambda: g.iota(ap(o), pattern, base, cm), [], [o])
 
+    def zero(o, n):
+        act(o, ("ones", 0, n), ACT.Copy, scale=0.0)
+
     def planes(dst, src, c0, n):
         for b in range(4):
             o, i = (dst, C * b + c0, C * b + c0 + n), (src, 4 * c0 + b, 4 * (c0 + n), 4)
@@ -300,12 +293,12 @@ def rank_program(g, core, T, topo):
     g.sync.dma_start(T.us[:], T.u[:]).then_inc(T.sem.ldu, 16)
     wrote([("us", 0, 512)], "ldu", 16)
     count["ldu"] = 16
-    for i, pcs in enumerate(PLAN["stages1"]):
-        lo, hi = 4 * PC * pcs[0], 4 * PC * (pcs[-1] + 1)
+    for i, hf in enumerate((up, 1 - up)):
+        lo, hi = 1024 * hf, 1024 * hf + 1024
         g.sync.dma_start(T.xs[:, lo:hi], T.x[:, lo:hi]).then_inc(T.sem["ldx%d" % i], 16)
         wrote([("xs", lo, hi)], "ldx%d" % i, 16)
         count["ldx%d" % i] = 16
-    wait("y", "ldx%d" % (len(PLAN["stages1"]) - 1), 16)
+    wait("y", "ldx1", 16)
     g.sync.dma_start(T.vs[:], T.v[:]).then_inc(T.sem.ldr, 16)
     g.sync.dma_start(T.ms[:], T.m[:]).then_inc(T.sem.ldr, 16)
     g.sync.dma_start(T.wqc[:].bitcast(dt.uint8), T.wc[:]).then_inc(T.sem.ldr, 16)
@@ -314,12 +307,10 @@ def rank_program(g, core, T, topo):
     count["ldr"] = 64
 
     hs = _helpers(T, topo, core)
-    far = topo.engines(core, T.cores[rank ^ 1])
-    both = topo.engines(core, hs[0])
-    near = [e for e in both if e not in far]
+    far = _engines(T, topo, core, 1)[0]
     for e, land, pair in ((1, "aa", "a"), (2, "bb", "b")):
         for k in range(4):
-            n = 2 * len(far) * (2 if (e == 1 and k == 3 and help1) else 1)
+            n = 2 * len(far) * (2 if (k and PLAN["route"][e - 1][k - 1] in "sn") else 1)
             count["a%d_%d" % (e, k)] = n
             if k:
                 name, c0, w = land, PC * (a0 ^ k), PC
@@ -336,6 +327,7 @@ def rank_program(g, core, T, topo):
     def send(e, k):
         src, land, pair = ("qf", "aa", "a") if e == 1 else ("qt", "bb", "b")
         sem = T.sem["a%d_%d" % (e, k)]
+        near, wide = _engines(T, topo, core, e)[1:]
         a = a0 ^ k
         for p in "cs":
             if k == 0:
@@ -345,19 +337,22 @@ def rank_program(g, core, T, topo):
                        _view(T, pair + "oe"[odd] + p, c0, c0 + RUN))]
             else:
                 need("g", [(src + p, PC * a, PC * a + PC)])
-                if e == 1 and k == 3 and help1:
-                    h = len(near) // 2
-                    mv = [(hs[j], near[h * j:h * j + h], T.sem["h1" + p],
-                           _view(T, src + p, PC * a + RUN * j, PC * a + RUN * j + RUN), _view(T, "h1" + p, 0, RUN))
-                          for j in range(2)]
-                elif e == 2 and k >= 2 and help2:
-                    mv = [(hs[k - 2], both, T.sem["h2" + p], _view(T, src + p, PC * a, PC * a + PC),
-                           _view(T, "h2" + p, 0, PC))]
+                how, hsem, hb = PLAN["route"][e - 1][k - 1], T.sem["h%d%d%s" % (e, k, p)], "h%d%s" % (e, p)
+                runs = [_view(T, src + p, PC * a + RUN * j, PC * a + RUN * j + RUN) for j in range(2)]
+                there = _view(T, land + p, RUN * rank, RUN * rank + RUN)
+                if how == "s":
+                    h = len(wide) // 2
+                    mv = [(hs[j], wide[h * j:h * j + h], hsem, runs[j],
+                           _view(T, hb, PC * k + RUN * j, PC * k + RUN * j + RUN)) for j in range(2)]
+                elif how == "n":
+                    mv = [(T.cores[2 * a], far, sem, runs[0], there),
+                          (hs[2], near, hsem, runs[1], _view(T, hb, PC * k + RUN, PC * k + PC))]
+                elif how != "d":
+                    mv = [(hs[int(how)], wide, hsem, _view(T, src + p, PC * a, PC * a + PC),
+                           _view(T, hb, PC * k, PC * k + PC))]
                 else:
                     h = len(far) // 2
-                    mv = [(T.cores[2 * a + j], far[h * j:h * j + h], sem,
-                           _view(T, src + p, PC * a + RUN * j, PC * a + RUN * j + RUN),
-                           _view(T, land + p, RUN * rank, RUN * rank + RUN)) for j in range(2)]
+                    mv = [(T.cores[2 * a + j], far[h * j:h * j + h], sem, runs[j], there) for j in range(2)]
             count["ls"] += _send(g, T, topo, mv, T.sem.ls)
 
     def arrived(e, k):
@@ -367,226 +362,192 @@ def rank_program(g, core, T, topo):
         c0 = PC * a0
         return "ab"[e - 1] + "eo"[odd], RUN * odd, [(0, c0 + RUN, RUN), (RUN, c0, RUN)]
 
-    H16, TWO, NEG, ADD, KOD = [("cols", i, i + 1) for i in range(5)]
+    H16, R16, NEG, ADD, KOD, KC = [("cols", i, i + 1) for i in range(6)]
     iota(("iu", 0, 8), [[16, 8]], 0, 0)
-    iota(("ia", 0, 256), [[1, 256]], 128, -1)
     iota(("ip", 0, 8), [[0, 8]], 0, 1)
+    iota(("ia", 0, 256), [[1, 256]], 128, -1)
+    iota(("mi", 0, 544), [[0, 17], [16, 2], [0, 16]], 0, 0, True)
     iota(("jsrc", 0, 512), [[1, 512]], -256, 0, True)
-    memset(("sa1", 0, 32 * NS), 0.0)
-    memset(("sob1", 255, 32 * 256, 256), 0.0)
-    copy(("offu", 0, 8), ("iu", 0, 8))
-    memset(("w1", 0, 544), 0.0)
     memset(("ones", 0, 512), 1.0)
-    ts(("ib", 0, 256), ("ia", 0, 256), 15, None, A.bitwise_and)
-    memset(("keepn", 0, 32 * NS), 1.0)
+    act(("mb", D - 1, D * C, D), ("ones", 0, C), ACT.Copy, scale=-1.0)
+    for t in range(16):
+        b = t + (0 if up else 16)
+        zero(("mb" if t // 8 else "ma", D * 16 * b + t % 8, D * 16 * (b + 1), D), 16)
+    for k in (("cs", 0, 16), ("cs", 528, 544), ("cum", 0, 16), ("w1", 0, 16)):
+        zero(k, 16)
+    zero(("w1", 512, 544), 32)
+    zero(("rv1", 127, 32 * 256, 128), 64)
+    zero(("ra1", 0, 64), 64)
+    zero(("rc1", 0, 4), 4)
+    copy(("offu", 0, 8), ("iu", 0, 8))
+    memset(("keep", 0, 256), 1.0)
     ts(("iq", 0, 8), ("ip", 0, 8), 16, None, A.bitwise_and)
-    ts(("pick", 0, 256), ("ib", 0, 256), 0.0, None, A.is_equal)
+    ts(("ir", 0, 8), ("ip", 0, 8), 15, None, A.bitwise_and)
+    memset(("keep", 0, 256, 16), 0.0)
     copy(H16, ("iq", 0, 1))
-    ts(("keep", 0, 256), ("ib", 0, 256), 0.0, None, A.not_equal)
-    memset(("keepn", 0, 32 * NS, NS), 0.0)
-    memset(("ksel", 0, 64), -4096.0)
-    ts(TWO, H16, 2.0, 512.0, A.mult, A.add)
+    copy(R16, ("ir", 0, 1))
+    ts(("ib", 0, 256), ("ia", 0, 256), 15, None, A.bitwise_and)
+    memset(("kc", 0, 16), 224.0 if up else -271.0)
+    memset(("kc", 16, 32), 240.0 if up else -287.0)
+    ts(("pick", 0, 256), ("ib", 0, 256), 0.0, None, A.is_equal)
+    ts(KC, H16, sg, R16, A.mult, A.add)
     ts(NEG, H16, -1.0, None, A.mult)
+    ts(("cm", 0, 256), ("pick", 0, 256), -2 * sg * BIG, sg * BIG, A.mult, A.add)
+    ts(("rst", 0, 256), ("pick", 0, 256), 2 * sg * BIG, -sg * BIG, A.mult, A.add)
+    ts(("kc", 0, 32), ("kc", 0, 32), KC, None, A.add)
+    memset(("rst", 0, 256, 16), sg * BIG)
+    spread("u")
     ts(ADD, H16, 64.0, -768.0, A.mult, A.add)
     ts(KOD, H16, -320.0, 1024.0, A.mult, A.add)
+    memset(("ksel", 0, 64), -4096.0)
+    ts(("mk", 0, 544), ("mi", 0, 544), H16, None, A.is_equal)
     ts(("ksel", 1, 64, 2), ("ksel", 0, 64, 2), 0.0, KOD, A.mult, A.add)
-    spread("u")
 
-    def sorter(n, nstage):
-        st = {"pv": None, "ps": None, "nv": 0, "ns": 0, "last": {}, "slot": {}, "have": [], "dv": [], "ds": [], "stage": 0,
-              "scalar": set(), "done": set(), "fin": set(), "tail": []}
-        r, sbn, sa, sx, w = "r" + n, "sb" + n, "sa" + n, "sx" + n, "w" + n
+    def sorter(n, wside, x):
+        st = {"pv": None, "ps": None, "ns": 0}
+        z = int(n) - 1
+        kv0, ks0 = PLAN["early"][z]
+        pv_, ps_ = PLAN["psum"]
+        sbn, w = "sb" + n, "w" + n
+        near_op, far_op = (A.is_gt, A.is_ge) if up else (A.is_lt, A.is_le)
+        mir = (lambda b: b) if up else (lambda b: 31 - b)
+
+        def unit(m, lo, hi):
+            lo, hi = sorted((mir(lo), mir(hi - 1)))
+            return mir(m), 16 * lo, 16 * hi + 16
+
+        first = [unit(m, m + 1, 32) for m in range(16, 31)]
+        longs = [unit(m, m + 1, m + 17) for m in range(16)]
+        wraps = [unit(m, 0, m - 16) for m in range(31, 16, -1)]
 
         def own(m):
             return (sbn, 16 * m + 15, 16 * m + 16)
 
-        def segments(m, pieces):
-            runs = []
-            for a in sorted(pieces):
-                if runs and runs[-1][1] == PC * a:
-                    runs[-1][1] += PC
-                else:
-                    runs.append([PC * a, PC * a + PC])
-            cut = 16 * m + 16
-            ge = [(lo, min(hi, cut), True) for lo, hi in runs if lo < cut]
-            gt = [(max(lo, cut), hi, False) for lo, hi in runs if hi > cut]
-            return runs, ge + gt
+        def slot(m, lo, hi):
+            return ("mb" if m % 16 // 8 else "ma", D * lo + m % 8, D * hi, D)
+
+        def scores(bank, c0, lo, hi, psum=True):
+            return ("ps", 512 * bank + lo - c0, 512 * bank + hi - c0) if psum else ("r" + n, lo, hi)
 
         def flush(which):
             if st[which]:
                 st[which]()
                 st[which] = None
 
-        def task_v(t):
-            m, pieces, stage = t
-            base = 512 * (st["nv"] % 4)
-            st["nv"] += 1
-            at = base
-            for lo, hi, tie in segments(m, pieces)[1]:
-                ts(("mv", at, at + hi - lo), (r, lo, hi), own(m), 0.5, A.is_ge if tie else A.is_gt, A.subtract)
-                at += hi - lo
+        def unit_v(u, bank, c0, how, end):
+            m, lo, hi = u
+            ts(slot(m, lo, hi), scores(bank, c0, lo, hi, pv_), own(m), None, how)
             flush("pv")
-            h = (at - base) // 2
-            so = ("sob" + n) if (nstage - 1 - stage) % 2 == 0 else "soa"
-            end = 256 * m + 256
-            def later():
-                scan((so, end - h, end), ("mv", base, base + h), ("mv", base + h, base + 2 * h),
-                     st["last"].get(m, 0.0), A.add, A.add)
-                st["last"][m] = (so, end - 1, end)
-                if stage == nstage - 1:
-                    st["fin"].add(m)
-            st["pv"] = later
+            mid = (lo + hi) // 2
+            if end:
+                st["pv"] = lambda: scan(("rv" + n, 256 * m + end - (mid - lo), 256 * m + end), slot(m, lo, mid),
+                                        slot(m, mid, hi), 0.0, A.add, A.add)
 
-        def task_s(t):
-            m, pieces, stage = t
-            base = 512 * (st["ns"] % 4)
+        def unit_s(u, bank, c0):
+            m, lo, hi = u
+            t = ("mt", 256 * (st["ns"] % 4), 256 * (st["ns"] % 4) + hi - lo)
             st["ns"] += 1
-            runs, segs = segments(m, pieces)
-            at = base
-            for lo, hi in runs:
-                act(("mt", at, at + hi - lo), (r, lo, hi), ACT.Sign, bias=own(m), scale=-1.0)
-                at += hi - lo
+            act(t, scores(bank, c0, lo, hi, ps_), ACT.Sign, bias=own(m), scale=-1.0)
             flush("ps")
-            mid = base + sum(hi - lo for lo, hi, tie in segs if tie)
-            def later():
-                for lo, hi, bias in ((base, mid, 0.5), (mid, at, -0.5)):
-                    if hi > lo:
-                        sl = st["slot"].get(m, 2)
-                        st["slot"][m] = sl + 1
-                        act(("mt", lo, hi), ("mt", lo, hi), ACT.Sign, bias=bias, scale=-1.0,
-                            acc=(sa, NS * m + sl, NS * m + sl + 1))
-            st["ps"] = later
+            st["ps"] = lambda: act(slot(m, lo, hi), t, ACT.Relu, scale=-sg, acc=("ra" + n, 2 * m, 2 * m + 1))
 
-        def fill_v(k):
-            for t in st["dv"][:k]:
-                task_v(t)
-            st["dv"] = st["dv"][k:]
+        def owned(hf, bank, c0):
+            lo, hi = 256 * hf, 256 * hf + 256
+            pv, gk = scores(bank, c0, lo, hi), ("ma", D * lo + D - 1, D * hi, D)
+            if not (pv_ and ps_):
+                copy(("r" + n, lo, hi), scores(bank + 1, c0, lo, hi), "s")
+            return [lambda: tt(("msk", 0, 256), pv, ("cm", 0, 256), A.max if up else A.min),
+                    lambda: scan((sbn, lo, hi), ("rst", 0, 256), ("msk", 0, 256), 0.0,
+                                 A.max if up else A.min, A.min if up else A.max),
+                    lambda: tt(gk, pv, (sbn, lo, hi), A.is_gt if up else A.is_le),
+                    lambda: scan(("gs" + n, lo, hi), ("keep", 0, 256), gk, 0.0, A.mult, A.add),
+                    lambda: tt(("ra" + n, 32 * hf + 1, 32 * hf + 32, 2), ("gs" + n, lo + 15, hi, 16),
+                               ("kc", 16 * hf, 16 * hf + 16), A.add)]
 
-        def chunk(ms):
-            ms = sorted(set(ms) - st["done"])
-            st["done"] |= set(ms)
-            runs = []
-            for m in ms:
-                if runs and runs[-1][1] == m:
-                    runs[-1][1] = m + 1
-                else:
-                    runs.append([m, m + 1])
-            win = (w, 0, 528)
-            def one():
-                assert all(m in st["scalar"] or m in st["fin"] for m in ms)
-                for lo, hi in runs:
-                    if not all(m in st["scalar"] for m in range(lo, hi)):
-                        ts((sa, NS * lo + 1, NS * hi, NS), ("sob" + n, 256 * lo + 255, 256 * hi, 256), 2.0, None, A.mult)
-            def two():
-                for lo, hi in runs:
-                    scan((sx, NS * lo, NS * hi), ("keepn", 0, NS * (hi - lo)), (sa, NS * lo, NS * hi), 0.0, A.mult, A.add)
-            def three():
-                for lo, hi in runs:
-                    ts(("pos" + n, lo, hi), (sx, NS * lo + NS - 1, NS * hi, NS), 0.5, None, A.mult)
-            def four():
-                for lo, hi in runs:
-                    off, src = ("pos" + n, lo, hi), ("jsrc", 16 * lo, 16 * hi)
-                    op("v", lambda: V.tensor_copy(ap(win).indirect(ap(off)), ap(src)), [off, src], [win])
-            return [one, two, three, four]
+        def stage_a():
+            c0 = 256 * up
+            mm(4, wside, 0, x, c0, 256)
+            mm(5, wside, 0, x, c0, 256)
+            steps = owned(up, 4, c0)
+            steps[0]()
+            steps[1]()
+            return ([lambda u=u: unit_s(u, 5, c0) for u in first[kv0:kv0 + ks0]],
+                    steps[2:] + [lambda u=u: unit_v(u, 4, c0, near_op, 128) for u in first[:kv0]])
 
-        def stage(pieces, shares, wside, x, late, copier, chunks=()):
-            s = st["stage"]
-            st["stage"] += 1
-            c0, wd = PC * min(pieces), PC * len(pieces)
-            bv, bs = 4 + s % 2, (6 if copier == "s" else 4) + s % 2
-            mm(bv, wside, 0, x, c0, wd)
-            if bs != bv:
-                mm(bs, wside, 0, x, c0, wd)
-            fill_v(99)
-            for t in st["ds"]:
-                task_s(t)
-            st["ds"] = []
-            copy((r, c0, c0 + wd), ("ps", 512 * bs, 512 * bs + wd), copier)
-            pv = ("ps", 512 * bv, 512 * bv + wd)
-            extras = [lambda: tt(("msk", 0, wd), pv, ("pick", 0, wd), A.mult),
-                      lambda: scan((sbn, c0, c0 + wd), ("keep", 0, wd), ("msk", 0, wd), 0.0, A.mult, A.add),
-                      lambda: tt(("eq", 0, wd), pv, (sbn, c0, c0 + wd), A.is_equal),
-                      lambda: scan(("eqs" + n, c0, c0 + wd), ("keep", 0, wd), ("eq", 0, wd), 0.0, A.mult, A.add)]
-            if s == nstage - 1:
-                extras.append(lambda: ts((sa, 0, 32 * NS, NS), ("eqs" + n, 15, C, 16), -2.0, TWO, A.mult, A.add))
-            old = [m for a in st["have"] for m in range(8 * a, 8 * a + 8)]
-            st["have"] = st["have"] + list(pieces)
-            new = []
-            for a, k in zip(pieces, shares):
-                new += list(range(8 * a, 8 * a + 8))
-                st["scalar"] |= set(range(8 * a + 8 - k, 8 * a + 8))
-            k = min(shares[-1], PLAN["tail"]) // 2 * 2
-            st["tail"] = list(range(8 * pieces[-1] + 8 - k, 8 * pieces[-1] + 8))
-            tasks = [(m, list(pieces), s) for m in old] + [(m, list(st["have"]), s) for m in new]
-            tv = [t for t in tasks if t[0] not in st["scalar"]]
-            tsc = [t for t in tasks if t[0] in st["scalar"]]
-            kv, ks = late
-            tv, st["dv"] = tv[:len(tv) - kv], tv[len(tv) - kv:]
-            tsc, st["ds"] = tsc[:len(tsc) - ks], tsc[len(tsc) - ks:]
-            if not old:
-                extras.pop(0)()
-                extras.pop(0)()
-            head = min(len(extras), len(tv))
-            for t in tv[:head]:
-                extras.pop(0)()
-                task_v(t)
-            for x_ in extras:
-                x_()
-            for t in tsc:
-                task_s(t)
-            if s == nstage - 1:
-                flush("ps")
-            steps = []
-            rest = tv[head:]
-            for i, t in enumerate(rest):
-                task_v(t)
-                for ms, before in chunks:
-                    if len(rest) - 1 - i == before:
-                        steps += chunk(ms)
-                for f in steps[:2]:
-                    f()
-                steps = steps[2:]
-            if s == nstage - 1:
-                flush("pv")
-            for f in steps:
-                f()
-
-        def finish():
-            for f in chunk([m for m in range(32) if m not in st["tail"]]) + chunk(st["tail"]):
-                f()
+        def stage_b(extra=()):
+            kv, sr = PLAN["vlong"][z], PLAN["sr"][z]
+            c0, wd = (0, C) if pv_ or ps_ else (256 * (1 - up), 256)
+            mm(6, wside, 0, x, c0, wd)
+            mm(7, wside, 0, x, c0, wd)
+            steps = owned(1 - up, 6, c0)
+            steps[0]()
+            steps[1]()
+            for u in longs[:16 - kv] + first[kv0 + ks0:]:
+                unit_s(u, 7, 0)
+            flush("ps")
+            steps = list(extra) + steps[2:]
+            for u in wraps:
+                unit_v(u, 6, 0, far_op, 256)
+                if steps:
+                    steps.pop(0)()
+            for i, u in enumerate(longs[16 - kv:]):
+                unit_v(u, 6, 0, near_op, 256 * (i < kv - sr))
+            flush("pv")
+            for i, (m, lo, hi) in enumerate(longs[16 - sr:]):
+                act(("mt", 256 * (i % 4), 256 * (i % 4) + 256), slot(m, lo, hi), ACT.Identity,
+                    acc=("ra" + n, 2 * m, 2 * m + 1))
+            for lo in range(0, C, CW) if up else reversed(range(0, C, CW)):
+                hi = min(C, lo + CW)
+                scan(("cum", 16 + D * lo, 16 + D * hi), ("ma", D * lo, D * hi), ("mb", D * lo, D * hi), CW - 256.0,
+                     A.add, A.add)
+            rc, ea, eb, ec, off = "rc" + n, ("ea" + n, 0, 32), ("eb" + n, 0, 32), ("ec" + n, 0, 32), ("pos" + n, 0, 32)
+            tt(("cs", 16, 16 + C), ("cum", 15 + D, 16 + D * C, D), ("cum", 15, 15 + D * C, D), A.subtract)
+            ts(("cs", 16, 16 + C, CW), ("cum", 15 + D, 16 + D * C, D * CW), 256.0 - CW, None, A.add)
+            turn(("ta", 0, C), ("cs", 16, 16 + C))
+            turn(("tb", 0, 544), ("cs", 0, 544))
+            scan(("xa", 0, C), ("ta", 0, C), ("mk", 0, C), 0.0, A.add, A.mult)
+            scan(("xb", 16, 16 + C), ("tb", 16, 16 + C), ("mk", 16, 16 + C), 0.0, A.add, A.mult)
+            scan((rc, 4, 68), ("rv" + n, 127, 32 * 256, 128), ("ra" + n, 0, 64), 0.0, A.add, A.add)
+            tt(eb, ("xa", 15, C, 16), ("xb", 31, C + 16, 16), A.add)
+            tt(ea, (rc, 5, 68, 2), (rc, 3, 66, 2), A.subtract)
+            tt(ec, ea, eb, A.subtract)
+            ts(off, ec, sg, None, A.mult)
+            win, src = (w, 0, 528), ("jsrc", 0, C)
+            op("v", lambda: V.tensor_copy(ap(win).indirect(ap(off)), ap(src)), [off, src], [win])
             tr, sel = "tr" + n, "sel" + n
-            ts(("plc" + n, 0, 32), (sx, NS - 1, 32 * NS, NS), 0.5, NEG, A.mult, A.add)
             for par in range(2):
-                o, i = (tr, 512 * par, 512 * par + 512), (w, 16 * par, 16 * par + 512)
-                op("v", lambda: V.transpose(ap(o), ap(i)), [i], [o])
+                turn((tr, 512 * par, 512 * par + 512), (w, 16 * par, 16 * par + 512))
+            ts(("plc" + n, 0, 32), ec, sg, NEG, A.mult, A.add)
             scan((sel, 0, 64), ("ksel", 0, 64), (tr, 0, 1024, 16), 0.0, A.add, A.max)
             for par in range(2):
                 ts(("ord" + n, par, 32, 2), (sel, 32 * par + 1, 32 * par + 32, 2), ADD, None, A.add)
 
-        def emit(out):
-            act(("out" + n, 0, 528), (w, 0, 528), ACT.Identity, bias=256.0)
-            for gr in range(8):
-                o = 16 * (gr % 2)
-                store("y", out[gr:gr + 1, :], T["out" + n][16 * gr:16 * gr + 1, o:o + C], [("out" + n, 0, 528)])
+        return stage_a, stage_b
 
-        return stage, fill_v, finish, emit
+    def emit(n, out):
+        act(("out" + n, 0, 528), ("w" + n, 0, 528), ACT.Identity, bias=256.0)
+        for k in range(4):
+            wait("y", "a%s_%d" % (n, k), count["a%s_%d" % (n, k)])
+        for gr in range(8):
+            o = 16 * (gr % 2)
+            store("y", out[gr:gr + 1, :], T["out" + n][16 * gr:16 * gr + 1, o:o + C], [("out" + n, 0, 528)])
 
-    last = len(PLAN["stages1"]) - 1
-    stage, fill_v, finish, emit = sorter("1", last + 1)
-    for i, pcs in enumerate(PLAN["stages1"]):
-        quant("qx", PC * pcs[0], PC * len(pcs), "xs", PC * pcs[0])
-        stage(list(pcs), [PLAN["share1"][a] for a in pcs], "ub", "qx", PLAN["late1"][i] if i < last else (0, 0),
-              PLAN["copy1"][i], [(range(hi), before) for hi, before in PLAN["chunks1"]] if i == last else ())
+    stage_a, stage_b = sorter("1", "ub", "qx")
+    quant("qx", 256 * up, 256, "xs", 256 * up)
+    for_s, for_v = stage_a()
+    for f in for_s + for_v:
+        f()
+    quant("qx", 256 * (1 - up), 256, "xs", 256 * (1 - up))
     planes("xp", "xs", 0, C)
     for b in range(4):
         o, i = ("et", 512 * b, 512 * b + 512), ("ones", 0, 512)
         op("g", lambda: g.affine_select(ap(o), ap(i), [[8, 128], [1, 4]], A.is_equal, 0.0, -b, -8), [i], [o])
-    finish()
+    stage_b()
 
     def move(q, tile, win, lst, c0, n, b):
         gather(q, (tile, 4 * c0 + b, 4 * (c0 + n), 4), (win, C * b, C * b + C), (lst, c0 // 16, (c0 + n) // 16))
 
-    order1 = PLAN["send1"]
+    order1 = PLAN["send"][0]
     mine = ((0, 1), (0, 1), (0,), (0, 1))
     for i, k in enumerate(order1):
         for b in range(4):
@@ -601,36 +562,46 @@ def rank_program(g, core, T, topo):
         if i in (0, 3):
             pack(1, k, "ft")
             send(1, k)
-    emit(T.oa)
+    emit("1", T.oa)
 
     spread("v")
-    memset(("sa2", 0, 32 * NS), 0.0)
-    memset(("sob2", 255, 32 * 256, 256), 0.0)
+    zero(("rv2", 127, 32 * 256, 128), 64)
+    zero(("ra2", 0, 64), 64)
+    zero(("rc2", 0, 4), 4)
     memset(("w2", 0, 544), 0.0)
     memset(("half", 0, 512), 0.5)
     quant("qm", 0, PC, "ms", 0)
     for b in range(4):
         quant("qe", PC * b, PC, "et", PC * b)
 
-    stage, fill_v, finish, emit = sorter("2", 4)
-    for k in range(4):
-        x, x0, parts = arrived(1, k)
+    def layer(s):
+        x, x0, parts = arrived(1, PLAN["proc"][s])
         for b in range(4):
             mm(b, "wq", PC * b, x, x0, PC)
         for b in (0, 2, 1, 3):
             for at, c0, wd in parts:
                 o, i = ("ht", 4 * c0 + b, 4 * (c0 + wd), 4), ("ps", 512 * b + at, 512 * b + at + wd)
-                if b in PLAN["evac"][k]:
+                if b in PLAN["evac"][s]:
                     act(o, i, ACT.Copy, scale=0.00390625)
                 else:
                     ts(o, i, 0.00390625, None, A.mult)
-        fill_v(1)
-        a = a0 ^ k
-        quant("qh", PC * a, PC, "ht", PC * a)
-        planes("hp", "ht", PC * a, PC)
-        stage([a], [PLAN["share2"][k]], "vb", "qh", PLAN["late2"][k] if k < 3 else (0, 0), PLAN["copy2"][k],
-              [([m for m in range(32) if m // 8 != a], PLAN["chunk2"])] if k == 3 else ())
-    finish()
+        quant("qh", PC * pieces[s], PC, "ht", PC * pieces[s])
+        planes("hp", "ht", PC * pieces[s], PC)
+
+    stage_a, stage_b = sorter("2", "vb", "qh")
+    for_s, for_v = [], []
+    for s in range(4):
+        layer(s)
+        if s == 1:
+            for_s, for_v = stage_a()
+        if s in (1, 2):
+            ks, kv = PLAN["between"][s - 1]
+            for f in for_s[:ks] + for_v[:kv]:
+                f()
+            for_s, for_v = for_s[ks:], for_v[kv:]
+    for f in for_s:
+        f()
+    stage_b(for_v)
 
     def sort_h(q, b, c0, n):
         gather(q, ("hs", C * b + c0, C * b + c0 + n), ("hp", C * b, C * b + C), ("ord2", c0 // 16, (c0 + n) // 16))
@@ -645,7 +616,7 @@ def rank_program(g, core, T, topo):
     sort_h("v", 3, 0, 256)
     for b in range(4):
         run(b)
-    order2 = PLAN["send2"]
+    order2 = PLAN["send"][1]
     mine = ((3,), (3,), (3, 2), (3, 2))
     for i, k in enumerate(order2):
         for b in range(4):
@@ -659,7 +630,7 @@ def rank_program(g, core, T, topo):
                 send(2, order2[i - 1])
     pack(2, order2[3], "tt")
     send(2, order2[3])
-    emit(T.ob)
+    emit("2", T.ob)
 
     comes = [("b" + "eo"[odd], RUN * (1 - odd), [(RUN * odd, PC * a0 + RUN * odd, RUN)])]
     for k in PLAN["home"]:

@@ -12,16 +12,17 @@ X4, U8 = "float8_e4m3fn_x4", "uint8"
 BF, F32, I32, U16 = "bfloat16", "float32", "int32", "uint16"
 
 PLAN = {
-    "vlong": (7, 7),
-    "sr": (6, 6),
-    "early": ((2, 4), (3, 3)),
-    "between": ((2, 5), (1, 0)),
-    "psum": (False, False),
-    "proc": (0, 1, 2, 3),
-    "evac": ((2, 3), (2, 3), (2, 3), (2, 3)),
+    "vlong": (6, 7),
+    "vfirst": (3, 3),
+    "vtail": (3, 2),
+    "sr": ((6, 4, 1), (7, 5, 0)),
+    "steps": (((4, 5),), ((0, 0), (1, 5), (2, 2))),
+    "pre": ((0, 2, 1), (2, 3, 1)),
+    "evac": ((2, 3), (2, 3), (1, 2, 3), (2, 3)),
     "route": ("dds", "d01"),
     "wide": (False, True),
-    "send": ((0, 1, 3, 2), (2, 3, 1, 0)),
+    "send": (((0,), (1, 3), (2,)), ((2,), (3,), (1,), (0,))),
+    "mine": (((0, 1), (0, 1), (0,), (0, 1)), ((3,), (3,), (3, 2), (3, 2))),
     "home": (1, 2, 3, 0),
     "out": (128, 384),
 }
@@ -31,9 +32,9 @@ def _scratch():
     s = {}
     def sb(n, w, d):
         s[n] = ("sbuf", [128, w], d)
-    for n in ("xs", "xp", "ft", "ht", "hp", "hs", "sc", "tt", "zs", "zt", "et"):
+    for n in ("xs", "xp", "ft", "ht", "hp", "hs", "sc", "tt", "zs", "zt"):
         sb(n, 4 * C, BF)
-    for n in ("us", "vs", "ms", "ones", "half", "jsrc"):
+    for n in ("us", "vs", "ms", "half", "jsrc"):
         sb(n, 512, BF)
     for n, w in (("qx", C), ("qu", PC), ("ub", PC), ("qv", PC), ("vb", PC), ("qm", PC), ("qe", C), ("wq", C),
                  ("qf", C), ("aa", C), ("ae", 192), ("ao", 192), ("qh", C), ("qt", C), ("bb", C), ("be", 192),
@@ -41,16 +42,16 @@ def _scratch():
         sb(n + "c", w, X4)
         sb(n + "s", w, U8)
     for n in ("1", "2"):
-        for k, w, d in (("r", C, F32), ("sb", C, F32), ("gs", C, BF), ("ra", 64, F32), ("rv", 32 * 256, BF), ("rc", 68, F32),
+        for k, w, d in (("r", C, F32), ("sb", C, F32), ("gs", C, BF), ("ra", 96, F32), ("rv", 32 * 384, BF), ("rc", 100, F32),
                         ("ea", 32, F32), ("eb", 32, F32), ("ec", 32, F32), ("w", 544, BF), ("tr", 1024, BF),
                         ("sel", 64, F32), ("pos", 32, U16), ("plc", 32, U16), ("ord", 32, U16), ("out", 528, F32)):
             sb(k + n, w, d)
     for k, w, d in (("ma", D * C, BF), ("mb", D * C, BF), ("cum", 16 + D * C, BF), ("cs", 544, BF), ("ta", 512, BF),
                     ("tb", 544, BF), ("xa", 512, BF), ("xb", 544, BF), ("mk", 544, BF), ("mi", 544, BF),
-                    ("msk", 256, F32), ("mt", 4 * 256, BF), ("ia", 256, I32), ("ib", 256, I32), ("pick", 256, BF),
-                    ("cm", 256, BF), ("rst", 256, BF), ("keep", 256, BF), ("kc", 32, F32), ("ksel", 64, F32),
-                    ("iu", 8, I32), ("offu", 8, U16), ("ip", 8, I32), ("iq", 8, I32), ("ir", 8, I32), ("cols", 8, F32),
-                    ("ys", C, F32)):
+                    ("msk", 256, F32), ("mt", 4 * 256, BF), ("e0", 520, BF), ("e1", 520, BF), ("ones", 520, BF),
+                    ("ia", 256, BF), ("pick", 256, BF), ("cm", 256, BF), ("rst", 256, BF), ("keep", 256, BF),
+                    ("kc", 32, F32), ("ksel", 64, F32), ("iu", 8, I32), ("offu", 8, U16), ("ip", 8, I32), ("iq", 8, I32),
+                    ("ir", 8, I32), ("cols", 8, F32), ("ys", C, F32)):
         sb(k, w, d)
     s["ps"] = ("psum", [128, 8 * 512], F32)
     return s
@@ -76,7 +77,7 @@ def _helpers(T, topo, home):
     ok = [c for c in topo.cores_of(home)
           if T.rank_of(c) is None and all(topo.may_write(c, d) for d in T.cores if d != c)]
     ok.sort(key=lambda c: (topo.die(c) == topo.die(home), c))
-    return ok[:3]
+    return ok[:2]
 
 
 def _view(T, name, a, b):
@@ -99,11 +100,24 @@ def _send(g, T, topo, moves, local):
     return sum(len(m[1]) for m in moves)
 
 
-def _engines(T, topo, home, e):
+def _ways(T, topo, home, e):
     far = topo.engines(home, T.cores[T.rank_of(home) ^ 1])
     both = topo.engines(home, _helpers(T, topo, home)[0])
     near = [x for x in both if x not in far]
-    return far, near, (both if PLAN["wide"][e - 1] else near)
+    out = {}
+    for call in PLAN["send"][e - 1]:
+        ws = []
+        for k in call:
+            how = PLAN["route"][e - 1][k - 1] if k else "m"
+            ws += [(k,) + w for w in {"m": [(0, None)], "d": [(0, None), (1, None)],
+                                      "s": [(0, 0), (1, 1)]}.get(how) or [(None, int(how))]]
+        direct = [w for w in ws if w[2] is None]
+        for part, pool in ((direct, far), ([w for w in ws if w[2] is not None],
+                                           both if PLAN["wide"][e - 1] and not direct else near)):
+            for i, w in enumerate(part):
+                n = len(pool) // len(part)
+                out.setdefault(w[0], []).append((w[1], w[2], pool[n * i:n * i + n]))
+    return out, far
 
 
 def _helper_program(g, core, T, topo):
@@ -118,20 +132,20 @@ def _helper_program(g, core, T, topo):
     far = topo.engines(core, T.cores[r ^ 2])
     total = 0
     for e in (1, 2):
-        near, wide = _engines(T, topo, home[0], e)[1:]
-        for k in PLAN["send"][e - 1]:
-            how = PLAN["route"][e - 1][k - 1] if k else "d"
-            js = {"s": [[0], [1], []][i], "n": [[], [], [1]][i], str(i): [0, 1]}.get(how)
-            if not js:
-                continue
-            a = (r // 2) ^ k
-            h = len(far) // len(js)
-            for p in "cs":
-                g.wait_ge(T.sem["h%d%d%s" % (e, k, p)], {"s": len(wide) // 2, "n": len(near)}.get(how, len(wide)))
-                total += _send(g, T, topo, [(T.cores[2 * a + j], far[h * n:h * n + h], T.sem["a%d_%d" % (e, k)],
-                                             _view(T, "h%d%s" % (e, p), PC * k + RUN * j, PC * k + RUN * j + RUN),
-                                             _view(T, ("aa", "bb")[e - 1] + p, RUN * r, RUN * r + RUN))
-                                            for n, j in enumerate(js)], T.sem.ls)
+        ways = _ways(T, topo, home[0], e)[0]
+        for k in [k for call in PLAN["send"][e - 1] for k in call]:
+            for j, h, eng in ways[k]:
+                if h != i:
+                    continue
+                a = (r // 2) ^ k
+                js = [0, 1] if j is None else [j]
+                n = len(far) // len(js)
+                for p in "cs":
+                    g.wait_ge(T.sem["h%d%d%s" % (e, k, p)], len(eng))
+                    total += _send(g, T, topo, [(T.cores[2 * a + j], far[n * t:n * t + n], T.sem["a%d_%d" % (e, k)],
+                                                 _view(T, "h%d%s" % (e, p), PC * k + RUN * j, PC * k + RUN * j + RUN),
+                                                 _view(T, ("aa", "bb")[e - 1] + p, RUN * r, RUN * r + RUN))
+                                                for t, j in enumerate(js)], T.sem.ls)
     if total:
         g.wait_ge(T.sem.ls, total)
 
@@ -142,9 +156,9 @@ def rank_program(g, core, T, topo):
         _helper_program(g, core, T, topo)
         return
     a0, odd = rank // 2, rank % 2
-    pieces = [a0 ^ k for k in PLAN["proc"]]
     up = a0 // 2
     sg = 1.0 if up else -1.0
+    halves = [(256 * h, 256 * h + 256) for h in (up, 1 - up)]
     queue = {"v": g.vector, "s": g.scalar, "p": g.tensor, "g": g, "y": g.sync}
     qsem = {"v": "sv", "s": "ss", "p": "sp", "g": "sg"}
     count = {"sv": 0, "ss": 0, "sp": 0, "sg": 0, "ls": 0, "st": 0}
@@ -257,7 +271,7 @@ def rank_program(g, core, T, topo):
             op("s", lambda: S.activation(ap(o), ap(win).indirect(ap(off)), ACT.Copy), [win, off], [o])
 
     def quant(name, c0, n, src, s0):
-        oc, os_, i = (name + "c", c0, c0 + n), (name + "s", c0, c0 + n), (src, 4 * s0, 4 * (s0 + n))
+        oc, os_, i = (name + "c", c0, c0 + n), (name + "s", c0, c0 + n), (src, s0, s0 + 4 * n)
         op("v", lambda: V.quantize_mx(ap(oc), ap(os_), ap(i)), [i], [oc, os_])
 
     def mm(bank, w, w0, x, x0, n):
@@ -290,13 +304,12 @@ def rank_program(g, core, T, topo):
         op("v", lambda: V.tensor_copy(ap(bc).bitcast(dt.uint32), ap(qc).bitcast(dt.uint32).indirect(ap(off))), [qc, off], [bc])
         gather("s", bs, qs, off)
 
-    g.sync.dma_start(T.us[:], T.u[:]).then_inc(T.sem.ldu, 16)
+    g.scalar.dma_start(T.us[:], T.u[:]).then_inc(T.sem.ldu, 16)
     wrote([("us", 0, 512)], "ldu", 16)
     count["ldu"] = 16
-    for i, hf in enumerate((up, 1 - up)):
-        lo, hi = 1024 * hf, 1024 * hf + 1024
-        g.sync.dma_start(T.xs[:, lo:hi], T.x[:, lo:hi]).then_inc(T.sem["ldx%d" % i], 16)
-        wrote([("xs", lo, hi)], "ldx%d" % i, 16)
+    for i, (lo, hi) in enumerate(halves):
+        g.sync.dma_start(T.xs[:, 4 * lo:4 * hi], T.x[:, 4 * lo:4 * hi]).then_inc(T.sem["ldx%d" % i], 16)
+        wrote([("xs", 4 * lo, 4 * hi)], "ldx%d" % i, 16)
         count["ldx%d" % i] = 16
     wait("y", "ldx1", 16)
     g.sync.dma_start(T.vs[:], T.v[:]).then_inc(T.sem.ldr, 16)
@@ -307,10 +320,12 @@ def rank_program(g, core, T, topo):
     count["ldr"] = 64
 
     hs = _helpers(T, topo, core)
-    far = _engines(T, topo, core, 1)[0]
+    ways = {e: _ways(T, topo, core, e) for e in (1, 2)}
     for e, land, pair in ((1, "aa", "a"), (2, "bb", "b")):
         for k in range(4):
-            n = 2 * len(far) * (2 if (k and PLAN["route"][e - 1][k - 1] in "sn") else 1)
+            far = ways[e][1]
+            n = [len(far) // 2 if j is None else len(eng if h is None else far)
+                 for j, h, eng in ways[e][0][k] if j in (None, odd if k else 0)][0] * (4 if k else 2)
             count["a%d_%d" % (e, k)] = n
             if k:
                 name, c0, w = land, PC * (a0 ^ k), PC
@@ -320,39 +335,37 @@ def rank_program(g, core, T, topo):
 
     def pack(e, k, tile):
         if k:
-            quant("qf" if e == 1 else "qt", PC * (a0 ^ k), PC, tile, PC * (a0 ^ k))
+            quant("qf" if e == 1 else "qt", PC * (a0 ^ k), PC, tile, 4 * PC * (a0 ^ k))
         else:
-            quant("ab"[e - 1] + "eo"[odd], RUN * (1 - odd), PC, tile, PC * a0)
+            quant("ab"[e - 1] + "eo"[odd], RUN * (1 - odd), PC, tile, 4 * PC * a0)
+
+    packed = set()
 
     def send(e, k):
         src, land, pair = ("qf", "aa", "a") if e == 1 else ("qt", "bb", "b")
-        sem = T.sem["a%d_%d" % (e, k)]
-        near, wide = _engines(T, topo, core, e)[1:]
-        a = a0 ^ k
+        packed.add((e, k))
+        call = [c for c in PLAN["send"][e - 1] if k in c][0]
+        if not all((e, c) in packed for c in call):
+            return
         for p in "cs":
-            if k == 0:
-                c0 = 128 * (1 - odd)
-                need("g", [(pair + "eo"[odd] + p, c0, c0 + RUN)])
-                mv = [(T.cores[rank ^ 1], far, sem, _view(T, pair + "eo"[odd] + p, c0, c0 + RUN),
-                       _view(T, pair + "oe"[odd] + p, c0, c0 + RUN))]
-            else:
-                need("g", [(src + p, PC * a, PC * a + PC)])
-                how, hsem, hb = PLAN["route"][e - 1][k - 1], T.sem["h%d%d%s" % (e, k, p)], "h%d%s" % (e, p)
-                runs = [_view(T, src + p, PC * a + RUN * j, PC * a + RUN * j + RUN) for j in range(2)]
-                there = _view(T, land + p, RUN * rank, RUN * rank + RUN)
-                if how == "s":
-                    h = len(wide) // 2
-                    mv = [(hs[j], wide[h * j:h * j + h], hsem, runs[j],
-                           _view(T, hb, PC * k + RUN * j, PC * k + RUN * j + RUN)) for j in range(2)]
-                elif how == "n":
-                    mv = [(T.cores[2 * a], far, sem, runs[0], there),
-                          (hs[2], near, hsem, runs[1], _view(T, hb, PC * k + RUN, PC * k + PC))]
-                elif how != "d":
-                    mv = [(hs[int(how)], wide, hsem, _view(T, src + p, PC * a, PC * a + PC),
-                           _view(T, hb, PC * k, PC * k + PC))]
-                else:
-                    h = len(far) // 2
-                    mv = [(T.cores[2 * a + j], far[h * j:h * j + h], sem, runs[j], there) for j in range(2)]
+            mv = []
+            for k in call:
+                a, sem = a0 ^ k, T.sem["a%d_%d" % (e, k)]
+                for j, h, eng in ways[e][0][k]:
+                    if k == 0:
+                        c0 = 128 * (1 - odd)
+                        need("g", [(pair + "eo"[odd] + p, c0, c0 + RUN)])
+                        mv.append((T.cores[rank ^ 1], eng, sem, _view(T, pair + "eo"[odd] + p, c0, c0 + RUN),
+                                   _view(T, pair + "oe"[odd] + p, c0, c0 + RUN)))
+                        continue
+                    lo, hi = (0, PC) if j is None else (RUN * j, RUN * j + RUN)
+                    need("g", [(src + p, PC * a, PC * a + PC)])
+                    run = _view(T, src + p, PC * a + lo, PC * a + hi)
+                    if h is None:
+                        mv.append((T.cores[2 * a + j], eng, sem, run, _view(T, land + p, RUN * rank, RUN * rank + RUN)))
+                    else:
+                        mv.append((hs[h], eng, T.sem["h%d%d%s" % (e, k, p)], run,
+                                   _view(T, "h%d%s" % (e, p), PC * k + lo, PC * k + hi)))
             count["ls"] += _send(g, T, topo, mv, T.sem.ls)
 
     def arrived(e, k):
@@ -365,20 +378,19 @@ def rank_program(g, core, T, topo):
     H16, R16, NEG, ADD, KOD, KC = [("cols", i, i + 1) for i in range(6)]
     iota(("iu", 0, 8), [[16, 8]], 0, 0)
     iota(("ip", 0, 8), [[0, 8]], 0, 1)
-    iota(("ia", 0, 256), [[1, 256]], 128, -1)
+    iota(("ia", 0, 256), [[0, 16], [1, 16]], 0, 0, True)
     iota(("mi", 0, 544), [[0, 17], [16, 2], [0, 16]], 0, 0, True)
+    iota(("kc", 0, 32), [[16 if up else -16, 2], [0, 16]], 224 if up else -271, 0, True)
     iota(("jsrc", 0, 512), [[1, 512]], -256, 0, True)
-    memset(("ones", 0, 512), 1.0)
-    act(("mb", D - 1, D * C, D), ("ones", 0, C), ACT.Copy, scale=-1.0)
+    for k in (("cs", 0, 16), ("cs", 528, 544), ("cum", 0, 16), ("w1", 0, 16), ("w1", 512, 544), ("rc1", 0, 4)):
+        iota(k, [[0, k[2] - k[1]]], 0, 0, True)
     for t in range(16):
         b = t + (0 if up else 16)
-        zero(("mb" if t // 8 else "ma", D * 16 * b + t % 8, D * 16 * (b + 1), D), 16)
-    for k in (("cs", 0, 16), ("cs", 528, 544), ("cum", 0, 16), ("w1", 0, 16)):
-        zero(k, 16)
-    zero(("w1", 512, 544), 32)
-    zero(("rv1", 127, 32 * 256, 128), 64)
-    zero(("ra1", 0, 64), 64)
-    zero(("rc1", 0, 4), 4)
+        iota(("mb" if t // 8 else "ma", D * 16 * b + t % 8, D * 16 * (b + 1), D), [[0, 16]], 0, 0, True)
+    memset(("ones", 0, 520), 1.0)
+    zero(("rv1", 127, 32 * 384, 128), 96)
+    zero(("ra1", 0, 96), 96)
+    act(("mb", D - 1, D * C, D), ("ones", 0, C), ACT.Copy, scale=-1.0)
     copy(("offu", 0, 8), ("iu", 0, 8))
     memset(("keep", 0, 256), 1.0)
     ts(("iq", 0, 8), ("ip", 0, 8), 16, None, A.bitwise_and)
@@ -386,28 +398,23 @@ def rank_program(g, core, T, topo):
     memset(("keep", 0, 256, 16), 0.0)
     copy(H16, ("iq", 0, 1))
     copy(R16, ("ir", 0, 1))
-    ts(("ib", 0, 256), ("ia", 0, 256), 15, None, A.bitwise_and)
-    memset(("kc", 0, 16), 224.0 if up else -271.0)
-    memset(("kc", 16, 32), 240.0 if up else -287.0)
-    ts(("pick", 0, 256), ("ib", 0, 256), 0.0, None, A.is_equal)
-    ts(KC, H16, sg, R16, A.mult, A.add)
-    ts(NEG, H16, -1.0, None, A.mult)
-    ts(("cm", 0, 256), ("pick", 0, 256), -2 * sg * BIG, sg * BIG, A.mult, A.add)
-    ts(("rst", 0, 256), ("pick", 0, 256), 2 * sg * BIG, -sg * BIG, A.mult, A.add)
-    ts(("kc", 0, 32), ("kc", 0, 32), KC, None, A.add)
-    memset(("rst", 0, 256, 16), sg * BIG)
-    spread("u")
-    ts(ADD, H16, 64.0, -768.0, A.mult, A.add)
     ts(KOD, H16, -320.0, 1024.0, A.mult, A.add)
+    ts(("pick", 0, 256), ("ia", 0, 256), R16, 0.5, A.is_equal, A.subtract)
     memset(("ksel", 0, 64), -4096.0)
-    ts(("mk", 0, 544), ("mi", 0, 544), H16, None, A.is_equal)
+    ts(("cm", 0, 256), ("pick", 0, 256), -2 * sg * BIG, None, A.mult)
+    ts(("rst", 0, 256), ("pick", 0, 256), 2 * sg * BIG, None, A.mult)
+    ts(KC, H16, sg, R16, A.mult, A.add)
+    memset(("rst", 0, 256, 16), sg * BIG)
+    ts(NEG, H16, -1.0, None, A.mult)
+    ts(ADD, H16, 64.0, -768.0, A.mult, A.add)
     ts(("ksel", 1, 64, 2), ("ksel", 0, 64, 2), 0.0, KOD, A.mult, A.add)
+    spread("u")
+    ts(("mk", 0, 544), ("mi", 0, 544), H16, None, A.is_equal)
 
-    def sorter(n, wside, x):
-        st = {"pv": None, "ps": None, "ns": 0}
+    def sorter(n, wside, x, parts, ahead, spare):
+        st = {"pv": None, "ps": None, "ns": 0, "late": []}
         z = int(n) - 1
-        kv0, ks0 = PLAN["early"][z]
-        pv_, ps_ = PLAN["psum"]
+        sr = PLAN["sr"][z]
         sbn, w = "sb" + n, "w" + n
         near_op, far_op = (A.is_gt, A.is_ge) if up else (A.is_lt, A.is_le)
         mir = (lambda b: b) if up else (lambda b: 31 - b)
@@ -426,129 +433,143 @@ def rank_program(g, core, T, topo):
         def slot(m, lo, hi):
             return ("mb" if m % 16 // 8 else "ma", D * lo + m % 8, D * hi, D)
 
-        def scores(bank, c0, lo, hi, psum=True):
-            return ("ps", 512 * bank + lo - c0, 512 * bank + hi - c0) if psum else ("r" + n, lo, hi)
-
         def flush(which):
             if st[which]:
                 st[which]()
                 st[which] = None
 
-        def unit_v(u, bank, c0, how, end):
+        def unit_v(u, how, end, late):
             m, lo, hi = u
-            ts(slot(m, lo, hi), scores(bank, c0, lo, hi, pv_), own(m), None, how)
+            ts(slot(m, lo, hi), ("r" + n, lo, hi), own(m), None, how)
             flush("pv")
             mid = (lo + hi) // 2
-            if end:
-                st["pv"] = lambda: scan(("rv" + n, 256 * m + end - (mid - lo), 256 * m + end), slot(m, lo, mid),
+            if late is not None:
+                st["late"].append((m, lo, hi, late))
+            else:
+                st["pv"] = lambda: scan(("rv" + n, 384 * m + end - (mid - lo), 384 * m + end), slot(m, lo, mid),
                                         slot(m, mid, hi), 0.0, A.add, A.add)
 
-        def unit_s(u, bank, c0):
+        def unit_s(u):
             m, lo, hi = u
             t = ("mt", 256 * (st["ns"] % 4), 256 * (st["ns"] % 4) + hi - lo)
             st["ns"] += 1
-            act(t, scores(bank, c0, lo, hi, ps_), ACT.Sign, bias=own(m), scale=-1.0)
+            act(t, ("r" + n, lo, hi), ACT.Sign, bias=own(m), scale=-1.0)
             flush("ps")
-            st["ps"] = lambda: act(slot(m, lo, hi), t, ACT.Relu, scale=-sg, acc=("ra" + n, 2 * m, 2 * m + 1))
+            st["ps"] = lambda: act(slot(m, lo, hi), t, ACT.Relu, scale=-sg, acc=("ra" + n, 3 * m, 3 * m + 1))
 
-        def owned(hf, bank, c0):
-            lo, hi = 256 * hf, 256 * hf + 256
-            pv, gk = scores(bank, c0, lo, hi), ("ma", D * lo + D - 1, D * hi, D)
-            if not (pv_ and ps_):
-                copy(("r" + n, lo, hi), scores(bank + 1, c0, lo, hi), "s")
-            return [lambda: tt(("msk", 0, 256), pv, ("cm", 0, 256), A.max if up else A.min),
-                    lambda: scan((sbn, lo, hi), ("rst", 0, 256), ("msk", 0, 256), 0.0,
-                                 A.max if up else A.min, A.min if up else A.max),
-                    lambda: tt(gk, pv, (sbn, lo, hi), A.is_gt if up else A.is_le),
+        def some(ks, kw):
+            for u in for_s[:ks]:
+                unit_s(u)
+            for f in for_v[:kw]:
+                f()
+            del for_s[:ks], for_v[:kw]
+
+        def owned(i):
+            lo, hi = halves[i]
+            b = 4 + 2 * i
+            mm(b, wside, 0, x, lo, 256)
+            mm(b + 1, wside, 0, x, lo, 256)
+            pv, gk = ("ps", 512 * b, 512 * b + 256), ("ma", D * lo + D - 1, D * hi, D)
+            if i:
+                some(*PLAN["pre"][z][:2])
+            copy(("r" + n, lo, hi), ("ps", 512 * b + 512, 512 * b + 768), "s")
+            tt(("msk", 0, 256), pv, ("cm", 0, 256), A.max if up else A.min)
+            if for_v or spare:
+                (for_v or spare).pop(0)()
+            scan((sbn, lo, hi), ("rst", 0, 256), ("msk", 0, 256), 0.0, A.max if up else A.min, A.min if up else A.max)
+            return [lambda: tt(gk, pv, (sbn, lo, hi), A.is_gt if up else A.is_le),
                     lambda: scan(("gs" + n, lo, hi), ("keep", 0, 256), gk, 0.0, A.mult, A.add),
-                    lambda: tt(("ra" + n, 32 * hf + 1, 32 * hf + 32, 2), ("gs" + n, lo + 15, hi, 16),
-                               ("kc", 16 * hf, 16 * hf + 16), A.add)]
+                    lambda: tt(("ra" + n, 3 * lo // 16 + 1, 3 * hi // 16, 3), ("gs" + n, lo + 15, hi, 16),
+                               ("kc", lo // 16, hi // 16), A.add)]
 
-        def stage_a():
-            c0 = 256 * up
-            mm(4, wside, 0, x, c0, 256)
-            mm(5, wside, 0, x, c0, 256)
-            steps = owned(up, 4, c0)
-            steps[0]()
-            steps[1]()
-            return ([lambda u=u: unit_s(u, 5, c0) for u in first[kv0:kv0 + ks0]],
-                    steps[2:] + [lambda u=u: unit_v(u, 4, c0, near_op, 128) for u in first[:kv0]])
-
-        def stage_b(extra=()):
-            kv, sr = PLAN["vlong"][z], PLAN["sr"][z]
-            c0, wd = (0, C) if pv_ or ps_ else (256 * (1 - up), 256)
-            mm(6, wside, 0, x, c0, wd)
-            mm(7, wside, 0, x, c0, wd)
-            steps = owned(1 - up, 6, c0)
-            steps[0]()
-            steps[1]()
-            for u in longs[:16 - kv] + first[kv0 + ks0:]:
-                unit_s(u, 7, 0)
-            flush("ps")
-            steps = list(extra) + steps[2:]
-            for u in wraps:
-                unit_v(u, 6, 0, far_op, 256)
-                if steps:
-                    steps.pop(0)()
-            for i, u in enumerate(longs[16 - kv:]):
-                unit_v(u, 6, 0, near_op, 256 * (i < kv - sr))
-            flush("pv")
-            for i, (m, lo, hi) in enumerate(longs[16 - sr:]):
-                act(("mt", 256 * (i % 4), 256 * (i % 4) + 256), slot(m, lo, hi), ACT.Identity,
-                    acc=("ra" + n, 2 * m, 2 * m + 1))
-            for lo in range(0, C, CW) if up else reversed(range(0, C, CW)):
-                hi = min(C, lo + CW)
-                scan(("cum", 16 + D * lo, 16 + D * hi), ("ma", D * lo, D * hi), ("mb", D * lo, D * hi), CW - 256.0,
-                     A.add, A.add)
-            rc, ea, eb, ec, off = "rc" + n, ("ea" + n, 0, 32), ("eb" + n, 0, 32), ("ec" + n, 0, 32), ("pos" + n, 0, 32)
-            tt(("cs", 16, 16 + C), ("cum", 15 + D, 16 + D * C, D), ("cum", 15, 15 + D * C, D), A.subtract)
-            ts(("cs", 16, 16 + C, CW), ("cum", 15 + D, 16 + D * C, D * CW), 256.0 - CW, None, A.add)
-            turn(("ta", 0, C), ("cs", 16, 16 + C))
-            turn(("tb", 0, 544), ("cs", 0, 544))
-            scan(("xa", 0, C), ("ta", 0, C), ("mk", 0, C), 0.0, A.add, A.mult)
-            scan(("xb", 16, 16 + C), ("tb", 16, 16 + C), ("mk", 16, 16 + C), 0.0, A.add, A.mult)
-            scan((rc, 4, 68), ("rv" + n, 127, 32 * 256, 128), ("ra" + n, 0, 64), 0.0, A.add, A.add)
-            tt(eb, ("xa", 15, C, 16), ("xb", 31, C + 16, 16), A.add)
-            tt(ea, (rc, 5, 68, 2), (rc, 3, 66, 2), A.subtract)
-            tt(ec, ea, eb, A.subtract)
-            ts(off, ec, sg, None, A.mult)
-            win, src = (w, 0, 528), ("jsrc", 0, C)
-            op("v", lambda: V.tensor_copy(ap(win).indirect(ap(off)), ap(src)), [off, src], [win])
-            tr, sel = "tr" + n, "sel" + n
-            for par in range(2):
-                turn((tr, 512 * par, 512 * par + 512), (w, 16 * par, 16 * par + 512))
-            ts(("plc" + n, 0, 32), ec, sg, NEG, A.mult, A.add)
-            scan((sel, 0, 64), ("ksel", 0, 64), (tr, 0, 1024, 16), 0.0, A.add, A.max)
-            for par in range(2):
-                ts(("ord" + n, par, 32, 2), (sel, 32 * par + 1, 32 * par + 32, 2), ADD, None, A.add)
-
-        return stage_a, stage_b
+        for_s, for_v, kv0, kv, vt = [], [], PLAN["vfirst"][z], PLAN["vlong"][z], 15 - PLAN["vtail"][z]
+        last = ([(u, far_op, 256, 2 if i >= 15 - sr[1] else None) for i, u in enumerate(wraps)]
+                + [(u, near_op, 256, 0 if i >= kv - sr[0] else None) for i, u in enumerate(longs[16 - kv:])])
+        for i, part in enumerate(parts):
+            ahead(i)
+            if part is not None:
+                steps = owned(part)
+                if part == 0:
+                    for_s += first[kv0:vt]
+                    for_v += [lambda u=u: unit_v(u, near_op, 128, None) for u in first[vt:]]
+                    for_v += [lambda u=u, j=j: unit_v(u, near_op, 128, 0 if j < sr[2] else None)
+                              for j, u in enumerate(first[:kv0])]
+                else:
+                    for_v[:0] = [lambda u=u: unit_v(*u) for u in last[:3]]
+                for j, f in enumerate(steps):
+                    for_v.insert(2 * j + 1, f)
+            if i < len(parts) - 1:
+                some(*PLAN["steps"][z][i])
+        lead = PLAN["pre"][z][2]
+        for u in for_s[:lead] + longs[:16 - kv] + for_s[lead:]:
+            unit_s(u)
+        flush("ps")
+        for f in for_v:
+            f()
+        for u in last[3:]:
+            unit_v(*u)
+        for f in spare:
+            f()
+        flush("pv")
+        for i, (m, lo, hi, at) in enumerate(st["late"]):
+            act(("mt", 256 * (i % 4), 256 * (i % 4) + hi - lo), slot(m, lo, hi), ACT.Identity,
+                acc=("ra" + n, 3 * m + at, 3 * m + at + 1))
+        for lo in range(0, C, CW) if up else reversed(range(0, C, CW)):
+            hi = min(C, lo + CW)
+            scan(("cum", 16 + D * lo, 16 + D * hi), ("ma", D * lo, D * hi), ("mb", D * lo, D * hi), CW - 256.0, A.add, A.add)
+        rc, ea, eb, ec, off = "rc" + n, "ea" + n, "eb" + n, "ec" + n, "pos" + n
+        sides = ((0, 9 * CW), (9 * CW, C)) if up else ((8 * CW, C), (0, 8 * CW))
+        for lo, hi in sides:
+            tt(("cs", 16 + lo, 16 + hi), ("cum", 15 + D * (lo + 1), 16 + D * hi, D), ("cum", 15 + D * lo, 15 + D * hi, D),
+               A.subtract)
+        for lo, hi in sides:
+            ts(("cs", 16 + lo, 16 + hi, CW), ("cum", 15 + D * (lo + 1), 16 + D * hi, D * CW), 256.0 - CW, None, A.add)
+        for lo, hi in halves[::-1]:
+            turn(("ta", lo, hi), ("cs", 16 + lo, 16 + hi))
+        turn(("tb", 0, 544), ("cs", 0, 544))
+        scan(("xa", 0, C), ("ta", 0, C), ("mk", 0, C), 0.0, A.add, A.mult)
+        scan(("xb", 16, 16 + C), ("tb", 16, 16 + C), ("mk", 16, 16 + C), 0.0, A.add, A.mult)
+        scan((rc, 4, 100), ("rv" + n, 127, 32 * 384, 128), ("ra" + n, 0, 96), 0.0, A.add, A.add)
+        tt((eb, 0, 32), ("xa", 15, C, 16), ("xb", 31, C + 16, 16), A.add)
+        for lo in (0, 16):
+            tt((ea, lo, lo + 16), (rc, 6 + 3 * lo, 52 + 3 * lo, 3), (rc, 3 + 3 * lo, 49 + 3 * lo, 3), A.subtract)
+        for lo in (0, 16):
+            tt((ec, lo, lo + 16), (ea, lo, lo + 16), (eb, lo, lo + 16), A.subtract)
+        for lo in (0, 16):
+            ts((off, lo, lo + 16), (ec, lo, lo + 16), sg, None, A.mult)
+        ts(("plc" + n, 0, 32), (ec, 0, 32), sg, NEG, A.mult, A.add)
+        win, o, src = (w, 0, 528), (off, 0, 32), ("jsrc", 0, C)
+        op("v", lambda: V.tensor_copy(ap(win).indirect(ap(o)), ap(src)), [o, src], [win])
+        tr, sel = "tr" + n, "sel" + n
+        for par in range(2):
+            turn((tr, 512 * par, 512 * par + 512), (w, 16 * par, 16 * par + 512))
+        for par in range(2):
+            scan((sel, 32 * par, 32 * par + 32), ("ksel", 0, 32), (tr, 512 * par, 512 * par + 512, 16), 0.0, A.add, A.max)
+        for par in range(2):
+            ts(("ord" + n, par, 32, 2), (sel, 32 * par + 1, 32 * par + 32, 2), ADD, None, A.add)
 
     def emit(n, out):
         act(("out" + n, 0, 528), ("w" + n, 0, 528), ACT.Identity, bias=256.0)
         for k in range(4):
             wait("y", "a%s_%d" % (n, k), count["a%s_%d" % (n, k)])
-        for gr in range(8):
-            o = 16 * (gr % 2)
-            store("y", out[gr:gr + 1, :], T["out" + n][16 * gr:16 * gr + 1, o:o + C], [("out" + n, 0, 528)])
+        for h in range(2):
+            store("y", out[h:8:2, :], T["out" + n][16 * h:128:32, 16 * h:16 * h + C], [("out" + n, 0, 528)])
 
-    stage_a, stage_b = sorter("1", "ub", "qx")
-    quant("qx", 256 * up, 256, "xs", 256 * up)
-    for_s, for_v = stage_a()
-    for f in for_s + for_v:
-        f()
-    quant("qx", 256 * (1 - up), 256, "xs", 256 * (1 - up))
-    planes("xp", "xs", 0, C)
-    for b in range(4):
-        o, i = ("et", 512 * b, 512 * b + 512), ("ones", 0, 512)
-        op("g", lambda: g.affine_select(ap(o), ap(i), [[8, 128], [1, 4]], A.is_equal, 0.0, -b, -8), [i], [o])
-    stage_b()
+    def load(i):
+        quant("qx", halves[i][0], 256, "xs", 4 * halves[i][0])
+        if i == 1:
+            planes("xp", "xs", 0, C)
+            for b in range(2):
+                o, k = ("e%d" % b, 0, 520), ("ones", 0, 520)
+                op("g", lambda: g.affine_select(ap(o), ap(k), [[1, 520]], A.is_equal, 0.0, -2 - b, -4), [k], [o])
+
+    sorter("1", "ub", "qx", (0, 1), load, [lambda: ts(("kc", 0, 32), ("kc", 0, 32), KC, None, A.add)])
 
     def move(q, tile, win, lst, c0, n, b):
         gather(q, (tile, 4 * c0 + b, 4 * (c0 + n), 4), (win, C * b, C * b + C), (lst, c0 // 16, (c0 + n) // 16))
 
-    order1 = PLAN["send"][0]
-    mine = ((0, 1), (0, 1), (0,), (0, 1))
+    order1 = [k for call in PLAN["send"][0] for k in call]
+    mine = PLAN["mine"][0]
     for i, k in enumerate(order1):
         for b in range(4):
             if b not in mine[i]:
@@ -565,43 +586,30 @@ def rank_program(g, core, T, topo):
     emit("1", T.oa)
 
     spread("v")
-    zero(("rv2", 127, 32 * 256, 128), 64)
-    zero(("ra2", 0, 64), 64)
+    zero(("rv2", 127, 32 * 384, 128), 96)
+    zero(("ra2", 0, 96), 96)
     zero(("rc2", 0, 4), 4)
-    memset(("w2", 0, 544), 0.0)
     memset(("half", 0, 512), 0.5)
     quant("qm", 0, PC, "ms", 0)
     for b in range(4):
-        quant("qe", PC * b, PC, "et", PC * b)
+        quant("qe", PC * b, PC, "e%d" % (b % 2), 2 - b // 2 * 2)
 
-    def layer(s):
-        x, x0, parts = arrived(1, PLAN["proc"][s])
-        for b in range(4):
+    def layer(k):
+        x, x0, parts = arrived(1, k)
+        for b in (0, 2, 1, 3):
             mm(b, "wq", PC * b, x, x0, PC)
         for b in (0, 2, 1, 3):
             for at, c0, wd in parts:
                 o, i = ("ht", 4 * c0 + b, 4 * (c0 + wd), 4), ("ps", 512 * b + at, 512 * b + at + wd)
-                if b in PLAN["evac"][s]:
+                if b in PLAN["evac"][k]:
                     act(o, i, ACT.Copy, scale=0.00390625)
                 else:
                     ts(o, i, 0.00390625, None, A.mult)
-        quant("qh", PC * pieces[s], PC, "ht", PC * pieces[s])
-        planes("hp", "ht", PC * pieces[s], PC)
+        quant("qh", PC * (a0 ^ k), PC, "ht", 4 * PC * (a0 ^ k))
+        planes("hp", "ht", PC * (a0 ^ k), PC)
 
-    stage_a, stage_b = sorter("2", "vb", "qh")
-    for_s, for_v = [], []
-    for s in range(4):
-        layer(s)
-        if s == 1:
-            for_s, for_v = stage_a()
-        if s in (1, 2):
-            ks, kv = PLAN["between"][s - 1]
-            for f in for_s[:ks] + for_v[:kv]:
-                f()
-            for_s, for_v = for_s[ks:], for_v[kv:]
-    for f in for_s:
-        f()
-    stage_b(for_v)
+    sorter("2", "vb", "qh", (None, 0, None, 1), layer,
+           [lambda: memset(("w2", 512, 544), 0.0), lambda: memset(("w2", 0, 16), 0.0)])
 
     def sort_h(q, b, c0, n):
         gather(q, ("hs", C * b + c0, C * b + c0 + n), ("hp", C * b, C * b + C), ("ord2", c0 // 16, (c0 + n) // 16))
@@ -616,8 +624,8 @@ def rank_program(g, core, T, topo):
     sort_h("v", 3, 0, 256)
     for b in range(4):
         run(b)
-    order2 = PLAN["send"][1]
-    mine = ((3,), (3,), (3, 2), (3, 2))
+    order2 = [k for call in PLAN["send"][1] for k in call]
+    mine = PLAN["mine"][1]
     for i, k in enumerate(order2):
         for b in range(4):
             if b not in mine[i]:
@@ -664,7 +672,7 @@ def rank_program(g, core, T, topo):
 
     def close(h):
         lo, hi = cuts[h], cuts[h + 1]
-        quant("qz", lo, hi - lo, "zt", lo)
+        quant("qz", lo, hi - lo, "zt", 4 * lo)
         store("y", T.oc[:, 4 * lo:4 * hi], _view(T, "qzc", lo, hi), [("qzc", lo, hi)])
 
     for h in range(nout):
@@ -681,7 +689,7 @@ def rank_program(g, core, T, topo):
         result(nout - 2)
     close(nout - 1)
     for k in range(4):
-        store("y", T.osc[4 * k:4 * k + 4, :], T.qzs[32 * k:32 * k + 4, :], [("qzs", 0, C)])
+        store("ys"[k % 2], T.osc[4 * k:4 * k + 4, :], T.qzs[32 * k:32 * k + 4, :], [("qzs", 0, C)])
     result(nout - 1)
 
     for sem, n in count.items():

import numpy as np
from concourse.bass import DstId, RemoteDMATransfer
from concourse.mybir import dt, AluOpType, ActivationFunctionType

C = 512
RUN = 64
PC = 128
D = 9
CW = 30
BIG = 2.0 ** 90
X4, U8 = "float8_e4m3fn_x4", "uint8"
BF, F32, I32, U16 = "bfloat16", "float32", "int32", "uint16"

PLAN = {
    "vlong": (6, 7),
    "vfirst": (3, 3),
    "vtail": (3, 2),
    "sr": ((6, 4, 1), (7, 5, 0)),
    "steps": (((4, 5),), ((0, 0), (1, 5), (2, 2))),
    "pre": ((0, 2, 1), (2, 3, 1)),
    "evac": ((2, 3), (2, 3), (1, 2, 3), (2, 3)),
    "route": ("dds", "d01"),
    "wide": (False, True),
    "send": (((0,), (1, 3), (2,)), ((2,), (3,), (1,), (0,))),
    "mine": (((0, 1), (0, 1), (0,), (0, 1)), ((3,), (3,), (3, 2), (3, 2))),
    "home": (1, 2, 3, 0),
    "out": (128, 384),
}


def _scratch():
    s = {}
    def sb(n, w, d):
        s[n] = ("sbuf", [128, w], d)
    for n in ("xs", "xp", "ft", "ht", "hp", "hs", "sc", "tt", "zs", "zt"):
        sb(n, 4 * C, BF)
    for n in ("us", "vs", "ms", "half", "jsrc"):
        sb(n, 512, BF)
    for n, w in (("qx", C), ("qu", PC), ("ub", PC), ("qv", PC), ("vb", PC), ("qm", PC), ("qe", C), ("wq", C),
                 ("qf", C), ("aa", C), ("ae", 192), ("ao", 192), ("qh", C), ("qt", C), ("bb", C), ("be", 192),
                 ("bo", 192), ("qz", C), ("h1", C), ("h2", C)):
        sb(n + "c", w, X4)
        sb(n + "s", w, U8)
    for n in ("1", "2"):
        for k, w, d in (("r", C, F32), ("sb", C, F32), ("gs", C, BF), ("ra", 96, F32), ("rv", 32 * 384, BF), ("rc", 100, F32),
                        ("ea", 32, F32), ("eb", 32, F32), ("ec", 32, F32), ("w", 544, BF), ("tr", 1024, BF),
                        ("sel", 64, F32), ("pos", 32, U16), ("plc", 32, U16), ("ord", 32, U16), ("out", 528, F32)):
            sb(k + n, w, d)
    for k, w, d in (("ma", D * C, BF), ("mb", D * C, BF), ("cum", 16 + D * C, BF), ("cs", 544, BF), ("ta", 512, BF),
                    ("tb", 544, BF), ("xa", 512, BF), ("xb", 544, BF), ("mk", 544, BF), ("mi", 544, BF),
                    ("msk", 256, F32), ("mt", 4 * 256, BF), ("e0", 520, BF), ("e1", 520, BF), ("ones", 520, BF),
                    ("ia", 256, BF), ("pick", 256, BF), ("cm", 256, BF), ("rst", 256, BF), ("keep", 256, BF),
                    ("kc", 32, F32), ("ksel", 64, F32), ("iu", 8, I32), ("offu", 8, U16), ("ip", 8, I32), ("iq", 8, I32),
                    ("ir", 8, I32), ("cols", 8, F32), ("ys", C, F32)):
        sb(k, w, d)
    s["ps"] = ("psum", [128, 8 * 512], F32)
    return s


SCRATCH = _scratch()
SEMAPHORES = (["sv", "ss", "sp", "sg", "ldu", "ldx0", "ldx1", "ldr", "ls", "st"]
              + ["a%d_%d" % (e, k) for e in (1, 2) for k in range(4)]
              + ["h%d%d%s" % (e, k, p) for e in (1, 2) for k in range(1, 4) for p in "cs"])

A = AluOpType
ACT = ActivationFunctionType


def _bits(engines):
    m = 0
    for e in engines:
        m |= 1 << e
    return m


def _helpers(T, topo, home):
    ok = [c for c in topo.cores_of(home)
          if T.rank_of(c) is None and all(topo.may_write(c, d) for d in T.cores if d != c)]
    ok.sort(key=lambda c: (topo.die(c) == topo.die(home), c))
    return ok[:2]


def _view(T, name, a, b):
    v = T[name][:, a:b]
    return v.bitcast(dt.uint8) if name.endswith("c") else v


def _send(g, T, topo, moves, local):
    if len(moves) == 1:
        d, eng, sem, src, dst = moves[0]
        rid, pid, se = topo.addr(d)
        g.remote_dma(dst, src, sem, local, pid, rid, _bits(eng))
    else:
        tr = []
        for d, eng, sem, src, dst in moves:
            rid, pid, se = topo.addr(d)
            tr.append(RemoteDMATransfer(dst_ids=[DstId(rid=rid, pnc=pid)], dma_engine_mask=_bits(eng),
                                        remote_sem=sem, src=src, dst=dst))
        g.remote_dma_fused(tr, local_sem=local)
    return sum(len(m[1]) for m in moves)


def _ways(T, topo, home, e):
    far = topo.engines(home, T.cores[T.rank_of(home) ^ 1])
    both = topo.engines(home, _helpers(T, topo, home)[0])
    near = [x for x in both if x not in far]
    out = {}
    for call in PLAN["send"][e - 1]:
        ws = []
        for k in call:
            how = PLAN["route"][e - 1][k - 1] if k else "m"
            ws += [(k,) + w for w in {"m": [(0, None)], "d": [(0, None), (1, None)],
                                      "s": [(0, 0), (1, 1)]}.get(how) or [(None, int(how))]]
        direct = [w for w in ws if w[2] is None]
        for part, pool in ((direct, far), ([w for w in ws if w[2] is not None],
                                           both if PLAN["wide"][e - 1] and not direct else near)):
            for i, w in enumerate(part):
                n = len(pool) // len(part)
                out.setdefault(w[0], []).append((w[1], w[2], pool[n * i:n * i + n]))
    return out, far


def _helper_program(g, core, T, topo):
    home = [c for c in T.cores if topo.chip(c) == topo.chip(core)]
    if not home:
        return
    hs = _helpers(T, topo, home[0])
    if core not in hs:
        return
    i = hs.index(core)
    r = T.rank_of(home[0])
    far = topo.engines(core, T.cores[r ^ 2])
    total = 0
    for e in (1, 2):
        ways = _ways(T, topo, home[0], e)[0]
        for k in [k for call in PLAN["send"][e - 1] for k in call]:
            for j, h, eng in ways[k]:
                if h != i:
                    continue
                a = (r // 2) ^ k
                js = [0, 1] if j is None else [j]
                n = len(far) // len(js)
                for p in "cs":
                    g.wait_ge(T.sem["h%d%d%s" % (e, k, p)], len(eng))
                    total += _send(g, T, topo, [(T.cores[2 * a + j], far[n * t:n * t + n], T.sem["a%d_%d" % (e, k)],
                                                 _view(T, "h%d%s" % (e, p), PC * k + RUN * j, PC * k + RUN * j + RUN),
                                                 _view(T, ("aa", "bb")[e - 1] + p, RUN * r, RUN * r + RUN))
                                                for t, j in enumerate(js)], T.sem.ls)
    if total:
        g.wait_ge(T.sem.ls, total)


def rank_program(g, core, T, topo):
    rank = T.rank_of(core)
    if rank is None:
        _helper_program(g, core, T, topo)
        return
    a0, odd = rank // 2, rank % 2
    up = a0 // 2
    sg = 1.0 if up else -1.0
    halves = [(256 * h, 256 * h + 256) for h in (up, 1 - up)]
    queue = {"v": g.vector, "s": g.scalar, "p": g.tensor, "g": g, "y": g.sync}
    qsem = {"v": "sv", "s": "ss", "p": "sp", "g": "sg"}
    count = {"sv": 0, "ss": 0, "sp": 0, "sg": 0, "ls": 0, "st": 0}
    waited = {q: {} for q in queue}
    tokens = [None]
    wr, rd = {}, {}
    for n, (where, shape, dty) in SCRATCH.items():
        w = 8 if where == "psum" else shape[1]
        wr[n] = np.zeros(w, np.int64)
        rd[n] = {q: np.zeros(w, np.int64) for q in qsem}

    def key(n, a, b, s=1):
        if n == "ps":
            return (n, slice(a // 512, (b - 1) // 512 + 1))
        return (n, slice(a, b, s))

    def ap(k):
        return T[k[0]][:, k[1]:k[2]:k[3]] if len(k) == 4 else T[k[0]][:, k[1]:k[2]]

    def wait(q, sem, val):
        if waited[q].get(sem, 0) < val:
            queue[q].wait_ge(T.sem[sem], int(val))
            waited[q][sem] = int(val)

    def need(q, reads, writes=()):
        want = {}
        def add(sem, val):
            if val > want.get(sem, 0):
                want[sem] = int(val)
        for k in list(reads) + list(writes):
            n, sl = key(*k)
            for t in np.unique(wr[n][sl]):
                if t:
                    add(*tokens[int(t)])
        for k in reads:
            if k[0] == "ps":
                n, sl = key(*k)
                for o in qsem:
                    if o != q:
                        add(qsem[o], rd[n][o][sl].max())
        for k in writes:
            n, sl = key(*k)
            for o in qsem:
                add(qsem[o], rd[n][o][sl].max())
        for sem, val in want.items():
            wait(q, sem, val)

    def wrote(keys, sem, val):
        tokens.append((sem, val))
        for k in keys:
            n, sl = key(*k)
            wr[n][sl] = len(tokens) - 1

    def op(q, make, reads, writes):
        need(q, reads, writes)
        sem = qsem[q]
        make().then_inc(T.sem[sem], 1)
        count[sem] += 1
        for k in reads:
            n, sl = key(*k)
            rd[n][q][sl] = count[sem]
        wrote(writes, sem, count[sem])

    V, S, P = g.vector, g.scalar, g.tensor

    def aps(*ks):
        return [k for k in ks if isinstance(k, tuple)]

    def val(k):
        return ap(k) if isinstance(k, tuple) else k

    def memset(o, c):
        op("v", lambda: V.memset(ap(o), c), [], [o])

    def ts(o, i, s1, s2, o0, o1=None):
        if o1 is None:
            op("v", lambda: V.tensor_scalar(ap(o), ap(i), val(s1), None, o0), aps(i, s1), [o])
        else:
            op("v", lambda: V.tensor_scalar(ap(o), ap(i), val(s1), val(s2), o0, o1), aps(i, s1, s2), [o])

    def tt(o, i0, i1, o0):
        op("v", lambda: V.tensor_tensor(ap(o), ap(i0), ap(i1), o0), [i0, i1], [o])

    def scan(o, d0, d1, init, o0, o1):
        op("v", lambda: V.tensor_tensor_scan(ap(o), ap(d0), ap(d1), val(init), o0, o1), aps(d0, d1, init), [o])

    def turn(o, i):
        op("v", lambda: V.transpose(ap(o), ap(i)), [i], [o])

    def act(o, i, func, bias=None, scale=None, acc=None):
        kw = {}
        if bias is not None:
            kw["bias"] = val(bias)
        if scale is not None:
            kw["scale"] = scale
        if acc is not None:
            kw["accum_out"] = ap(acc)
        op("s", lambda: S.activation(ap(o), ap(i), func, **kw), aps(i, bias), aps(o, acc))

    def copy(o, i, q="v"):
        if q == "v":
            op("v", lambda: V.tensor_copy(ap(o), ap(i)), [i], [o])
        else:
            act(o, i, ACT.Copy)

    def gather(q, o, win, off):
        if q == "v":
            op("v", lambda: V.tensor_copy(ap(o), ap(win).indirect(ap(off))), [win, off], [o])
        else:
            op("s", lambda: S.activation(ap(o), ap(win).indirect(ap(off)), ACT.Copy), [win, off], [o])

    def quant(name, c0, n, src, s0):
        oc, os_, i = (name + "c", c0, c0 + n), (name + "s", c0, c0 + n), (src, s0, s0 + 4 * n)
        op("v", lambda: V.quantize_mx(ap(oc), ap(os_), ap(i)), [i], [oc, os_])

    def mm(bank, w, w0, x, x0, n):
        ks = [(w + "c", w0, w0 + PC), (w + "s", w0, w0 + PC), (x + "c", x0, x0 + n), (x + "s", x0, x0 + n)]
        o = ("ps", 512 * bank, 512 * bank + n)
        op("p", lambda: P.matmul_mx(ap(o), ap(ks[0]), ap(ks[1]), ap(ks[2]), ap(ks[3]), True, True), ks, [o])

    def iota(o, pattern, base, cm, loose=False):
        if loose:
            op("g", lambda: g.iota(ap(o), pattern, base, cm, allow_small_or_imprecise_dtypes=True), [], [o])
        else:
            op("g", lambda: g.iota(ap(o), pattern, base, cm), [], [o])

    def zero(o, n):
        act(o, ("ones", 0, n), ACT.Copy, scale=0.0)

    def planes(dst, src, c0, n):
        for b in range(4):
            o, i = (dst, C * b + c0, C * b + c0 + n), (src, 4 * c0 + b, 4 * (c0 + n), 4)
            op("g", lambda: g.affine_select(ap(o), ap(i), [[0, n]], A.is_ge, 0.0, 0, 0), [i], [o])

    def store(q, out, src, reads):
        need(q, reads)
        queue[q].dma_start(out, src).then_inc(T.sem.st, 16)
        count["st"] += 16

    def spread(n):
        qc, qs, bc, bs, off = ("q" + n + "c", 0, PC), ("q" + n + "s", 0, PC), (n + "bc", 0, PC), (n + "bs", 0, PC), ("offu", 0, 8)
        quant("q" + n, 0, PC, n + "s", 0)
        op("v", lambda: V.tensor_copy(ap(bc).bitcast(dt.uint32), ap(qc).bitcast(dt.uint32).indirect(ap(off))), [qc, off], [bc])
        gather("s", bs, qs, off)

    g.scalar.dma_start(T.us[:], T.u[:]).then_inc(T.sem.ldu, 16)
    wrote([("us", 0, 512)], "ldu", 16)
    count["ldu"] = 16
    for i, (lo, hi) in enumerate(halves):
        g.sync.dma_start(T.xs[:, 4 * lo:4 * hi], T.x[:, 4 * lo:4 * hi]).then_inc(T.sem["ldx%d" % i], 16)
        wrote([("xs", 4 * lo, 4 * hi)], "ldx%d" % i, 16)
        count["ldx%d" % i] = 16
    wait("y", "ldx1", 16)
    g.sync.dma_start(T.vs[:], T.v[:]).then_inc(T.sem.ldr, 16)
    g.sync.dma_start(T.ms[:], T.m[:]).then_inc(T.sem.ldr, 16)
    g.sync.dma_start(T.wqc[:].bitcast(dt.uint8), T.wc[:]).then_inc(T.sem.ldr, 16)
    g.sync.dma_start(T.wqs[:], T.ws[:]).then_inc(T.sem.ldr, 16)
    wrote([("vs", 0, 512), ("ms", 0, 512), ("wqc", 0, C), ("wqs", 0, C)], "ldr", 64)
    count["ldr"] = 64

    hs = _helpers(T, topo, core)
    ways = {e: _ways(T, topo, core, e) for e in (1, 2)}
    for e, land, pair in ((1, "aa", "a"), (2, "bb", "b")):
        for k in range(4):
            far = ways[e][1]
            n = [len(far) // 2 if j is None else len(eng if h is None else far)
                 for j, h, eng in ways[e][0][k] if j in (None, odd if k else 0)][0] * (4 if k else 2)
            count["a%d_%d" % (e, k)] = n
            if k:
                name, c0, w = land, PC * (a0 ^ k), PC
            else:
                name, c0, w = pair + "eo"[odd], 128 * odd, RUN
            wrote([(name + "c", c0, c0 + w), (name + "s", c0, c0 + w)], "a%d_%d" % (e, k), n)

    def pack(e, k, tile):
        if k:
            quant("qf" if e == 1 else "qt", PC * (a0 ^ k), PC, tile, 4 * PC * (a0 ^ k))
        else:
            quant("ab"[e - 1] + "eo"[odd], RUN * (1 - odd), PC, tile, 4 * PC * a0)

    packed = set()

    def send(e, k):
        src, land, pair = ("qf", "aa", "a") if e == 1 else ("qt", "bb", "b")
        packed.add((e, k))
        call = [c for c in PLAN["send"][e - 1] if k in c][0]
        if not all((e, c) in packed for c in call):
            return
        for p in "cs":
            mv = []
            for k in call:
                a, sem = a0 ^ k, T.sem["a%d_%d" % (e, k)]
                for j, h, eng in ways[e][0][k]:
                    if k == 0:
                        c0 = 128 * (1 - odd)
                        need("g", [(pair + "eo"[odd] + p, c0, c0 + RUN)])
                        mv.append((T.cores[rank ^ 1], eng, sem, _view(T, pair + "eo"[odd] + p, c0, c0 + RUN),
                                   _view(T, pair + "oe"[odd] + p, c0, c0 + RUN)))
                        continue
                    lo, hi = (0, PC) if j is None else (RUN * j, RUN * j + RUN)
                    need("g", [(src + p, PC * a, PC * a + PC)])
                    run = _view(T, src + p, PC * a + lo, PC * a + hi)
                    if h is None:
                        mv.append((T.cores[2 * a + j], eng, sem, run, _view(T, land + p, RUN * rank, RUN * rank + RUN)))
                    else:
                        mv.append((hs[h], eng, T.sem["h%d%d%s" % (e, k, p)], run,
                                   _view(T, "h%d%s" % (e, p), PC * k + lo, PC * k + hi)))
            count["ls"] += _send(g, T, topo, mv, T.sem.ls)

    def arrived(e, k):
        if k:
            c0 = PC * (a0 ^ k)
            return ("aa" if e == 1 else "bb"), c0, [(0, c0, PC)]
        c0 = PC * a0
        return "ab"[e - 1] + "eo"[odd], RUN * odd, [(0, c0 + RUN, RUN), (RUN, c0, RUN)]

    H16, R16, NEG, ADD, KOD, KC = [("cols", i, i + 1) for i in range(6)]
    iota(("iu", 0, 8), [[16, 8]], 0, 0)
    iota(("ip", 0, 8), [[0, 8]], 0, 1)
    iota(("ia", 0, 256), [[0, 16], [1, 16]], 0, 0, True)
    iota(("mi", 0, 544), [[0, 17], [16, 2], [0, 16]], 0, 0, True)
    iota(("kc", 0, 32), [[16 if up else -16, 2], [0, 16]], 224 if up else -271, 0, True)
    iota(("jsrc", 0, 512), [[1, 512]], -256, 0, True)
    for k in (("cs", 0, 16), ("cs", 528, 544), ("cum", 0, 16), ("w1", 0, 16), ("w1", 512, 544), ("rc1", 0, 4)):
        iota(k, [[0, k[2] - k[1]]], 0, 0, True)
    for t in range(16):
        b = t + (0 if up else 16)
        iota(("mb" if t // 8 else "ma", D * 16 * b + t % 8, D * 16 * (b + 1), D), [[0, 16]], 0, 0, True)
    memset(("ones", 0, 520), 1.0)
    zero(("rv1", 127, 32 * 384, 128), 96)
    zero(("ra1", 0, 96), 96)
    act(("mb", D - 1, D * C, D), ("ones", 0, C), ACT.Copy, scale=-1.0)
    copy(("offu", 0, 8), ("iu", 0, 8))
    memset(("keep", 0, 256), 1.0)
    ts(("iq", 0, 8), ("ip", 0, 8), 16, None, A.bitwise_and)
    ts(("ir", 0, 8), ("ip", 0, 8), 15, None, A.bitwise_and)
    memset(("keep", 0, 256, 16), 0.0)
    copy(H16, ("iq", 0, 1))
    copy(R16, ("ir", 0, 1))
    ts(KOD, H16, -320.0, 1024.0, A.mult, A.add)
    ts(("pick", 0, 256), ("ia", 0, 256), R16, 0.5, A.is_equal, A.subtract)
    memset(("ksel", 0, 64), -4096.0)
    ts(("cm", 0, 256), ("pick", 0, 256), -2 * sg * BIG, None, A.mult)
    ts(("rst", 0, 256), ("pick", 0, 256), 2 * sg * BIG, None, A.mult)
    ts(KC, H16, sg, R16, A.mult, A.add)
    memset(("rst", 0, 256, 16), sg * BIG)
    ts(NEG, H16, -1.0, None, A.mult)
    ts(ADD, H16, 64.0, -768.0, A.mult, A.add)
    ts(("ksel", 1, 64, 2), ("ksel", 0, 64, 2), 0.0, KOD, A.mult, A.add)
    spread("u")
    ts(("mk", 0, 544), ("mi", 0, 544), H16, None, A.is_equal)

    def sorter(n, wside, x, parts, ahead, spare):
        st = {"pv": None, "ps": None, "ns": 0, "late": []}
        z = int(n) - 1
        sr = PLAN["sr"][z]
        sbn, w = "sb" + n, "w" + n
        near_op, far_op = (A.is_gt, A.is_ge) if up else (A.is_lt, A.is_le)
        mir = (lambda b: b) if up else (lambda b: 31 - b)

        def unit(m, lo, hi):
            lo, hi = sorted((mir(lo), mir(hi - 1)))
            return mir(m), 16 * lo, 16 * hi + 16

        first = [unit(m, m + 1, 32) for m in range(16, 31)]
        longs = [unit(m, m + 1, m + 17) for m in range(16)]
        wraps = [unit(m, 0, m - 16) for m in range(31, 16, -1)]

        def own(m):
            return (sbn, 16 * m + 15, 16 * m + 16)

        def slot(m, lo, hi):
            return ("mb" if m % 16 // 8 else "ma", D * lo + m % 8, D * hi, D)

        def flush(which):
            if st[which]:
                st[which]()
                st[which] = None

        def unit_v(u, how, end, late):
            m, lo, hi = u
            ts(slot(m, lo, hi), ("r" + n, lo, hi), own(m), None, how)
            flush("pv")
            mid = (lo + hi) // 2
            if late is not None:
                st["late"].append((m, lo, hi, late))
            else:
                st["pv"] = lambda: scan(("rv" + n, 384 * m + end - (mid - lo), 384 * m + end), slot(m, lo, mid),
                                        slot(m, mid, hi), 0.0, A.add, A.add)

        def unit_s(u):
            m, lo, hi = u
            t = ("mt", 256 * (st["ns"] % 4), 256 * (st["ns"] % 4) + hi - lo)
            st["ns"] += 1
            act(t, ("r" + n, lo, hi), ACT.Sign, bias=own(m), scale=-1.0)
            flush("ps")
            st["ps"] = lambda: act(slot(m, lo, hi), t, ACT.Relu, scale=-sg, acc=("ra" + n, 3 * m, 3 * m + 1))

        def some(ks, kw):
            for u in for_s[:ks]:
                unit_s(u)
            for f in for_v[:kw]:
                f()
            del for_s[:ks], for_v[:kw]

        def owned(i):
            lo, hi = halves[i]
            b = 4 + 2 * i
            mm(b, wside, 0, x, lo, 256)
            mm(b + 1, wside, 0, x, lo, 256)
            pv, gk = ("ps", 512 * b, 512 * b + 256), ("ma", D * lo + D - 1, D * hi, D)
            if i:
                some(*PLAN["pre"][z][:2])
            copy(("r" + n, lo, hi), ("ps", 512 * b + 512, 512 * b + 768), "s")
            tt(("msk", 0, 256), pv, ("cm", 0, 256), A.max if up else A.min)
            if for_v or spare:
                (for_v or spare).pop(0)()
            scan((sbn, lo, hi), ("rst", 0, 256), ("msk", 0, 256), 0.0, A.max if up else A.min, A.min if up else A.max)
            return [lambda: tt(gk, pv, (sbn, lo, hi), A.is_gt if up else A.is_le),
                    lambda: scan(("gs" + n, lo, hi), ("keep", 0, 256), gk, 0.0, A.mult, A.add),
                    lambda: tt(("ra" + n, 3 * lo // 16 + 1, 3 * hi // 16, 3), ("gs" + n, lo + 15, hi, 16),
                               ("kc", lo // 16, hi // 16), A.add)]

        for_s, for_v, kv0, kv, vt = [], [], PLAN["vfirst"][z], PLAN["vlong"][z], 15 - PLAN["vtail"][z]
        last = ([(u, far_op, 256, 2 if i >= 15 - sr[1] else None) for i, u in enumerate(wraps)]
                + [(u, near_op, 256, 0 if i >= kv - sr[0] else None) for i, u in enumerate(longs[16 - kv:])])
        for i, part in enumerate(parts):
            ahead(i)
            if part is not None:
                steps = owned(part)
                if part == 0:
                    for_s += first[kv0:vt]
                    for_v += [lambda u=u: unit_v(u, near_op, 128, None) for u in first[vt:]]
                    for_v += [lambda u=u, j=j: unit_v(u, near_op, 128, 0 if j < sr[2] else None)
                              for j, u in enumerate(first[:kv0])]
                else:
                    for_v[:0] = [lambda u=u: unit_v(*u) for u in last[:3]]
                for j, f in enumerate(steps):
                    for_v.insert(2 * j + 1, f)
            if i < len(parts) - 1:
                some(*PLAN["steps"][z][i])
        lead = PLAN["pre"][z][2]
        for u in for_s[:lead] + longs[:16 - kv] + for_s[lead:]:
            unit_s(u)
        flush("ps")
        for f in for_v:
            f()
        for u in last[3:]:
            unit_v(*u)
        for f in spare:
            f()
        flush("pv")
        for i, (m, lo, hi, at) in enumerate(st["late"]):
            act(("mt", 256 * (i % 4), 256 * (i % 4) + hi - lo), slot(m, lo, hi), ACT.Identity,
                acc=("ra" + n, 3 * m + at, 3 * m + at + 1))
        for lo in range(0, C, CW) if up else reversed(range(0, C, CW)):
            hi = min(C, lo + CW)
            scan(("cum", 16 + D * lo, 16 + D * hi), ("ma", D * lo, D * hi), ("mb", D * lo, D * hi), CW - 256.0, A.add, A.add)
        rc, ea, eb, ec, off = "rc" + n, "ea" + n, "eb" + n, "ec" + n, "pos" + n
        sides = ((0, 9 * CW), (9 * CW, C)) if up else ((8 * CW, C), (0, 8 * CW))
        for lo, hi in sides:
            tt(("cs", 16 + lo, 16 + hi), ("cum", 15 + D * (lo + 1), 16 + D * hi, D), ("cum", 15 + D * lo, 15 + D * hi, D),
               A.subtract)
        for lo, hi in sides:
            ts(("cs", 16 + lo, 16 + hi, CW), ("cum", 15 + D * (lo + 1), 16 + D * hi, D * CW), 256.0 - CW, None, A.add)
        for lo, hi in halves[::-1]:
            turn(("ta", lo, hi), ("cs", 16 + lo, 16 + hi))
        turn(("tb", 0, 544), ("cs", 0, 544))
        scan(("xa", 0, C), ("ta", 0, C), ("mk", 0, C), 0.0, A.add, A.mult)
        scan(("xb", 16, 16 + C), ("tb", 16, 16 + C), ("mk", 16, 16 + C), 0.0, A.add, A.mult)
        scan((rc, 4, 100), ("rv" + n, 127, 32 * 384, 128), ("ra" + n, 0, 96), 0.0, A.add, A.add)
        tt((eb, 0, 32), ("xa", 15, C, 16), ("xb", 31, C + 16, 16), A.add)
        for lo in (0, 16):
            tt((ea, lo, lo + 16), (rc, 6 + 3 * lo, 52 + 3 * lo, 3), (rc, 3 + 3 * lo, 49 + 3 * lo, 3), A.subtract)
        for lo in (0, 16):
            tt((ec, lo, lo + 16), (ea, lo, lo + 16), (eb, lo, lo + 16), A.subtract)
        for lo in (0, 16):
            ts((off, lo, lo + 16), (ec, lo, lo + 16), sg, None, A.mult)
        ts(("plc" + n, 0, 32), (ec, 0, 32), sg, NEG, A.mult, A.add)
        win, o, src = (w, 0, 528), (off, 0, 32), ("jsrc", 0, C)
        op("v", lambda: V.tensor_copy(ap(win).indirect(ap(o)), ap(src)), [o, src], [win])
        tr, sel = "tr" + n, "sel" + n
        for par in range(2):
            turn((tr, 512 * par, 512 * par + 512), (w, 16 * par, 16 * par + 512))
        for par in range(2):
            scan((sel, 32 * par, 32 * par + 32), ("ksel", 0, 32), (tr, 512 * par, 512 * par + 512, 16), 0.0, A.add, A.max)
        for par in range(2):
            ts(("ord" + n, par, 32, 2), (sel, 32 * par + 1, 32 * par + 32, 2), ADD, None, A.add)

    def emit(n, out):
        act(("out" + n, 0, 528), ("w" + n, 0, 528), ACT.Identity, bias=256.0)
        for k in range(4):
            wait("y", "a%s_%d" % (n, k), count["a%s_%d" % (n, k)])
        for h in range(2):
            store("y", out[h:8:2, :], T["out" + n][16 * h:128:32, 16 * h:16 * h + C], [("out" + n, 0, 528)])

    def load(i):
        quant("qx", halves[i][0], 256, "xs", 4 * halves[i][0])
        if i == 1:
            planes("xp", "xs", 0, C)
            for b in range(2):
                o, k = ("e%d" % b, 0, 520), ("ones", 0, 520)
                op("g", lambda: g.affine_select(ap(o), ap(k), [[1, 520]], A.is_equal, 0.0, -2 - b, -4), [k], [o])

    sorter("1", "ub", "qx", (0, 1), load, [lambda: ts(("kc", 0, 32), ("kc", 0, 32), KC, None, A.add)])

    def move(q, tile, win, lst, c0, n, b):
        gather(q, (tile, 4 * c0 + b, 4 * (c0 + n), 4), (win, C * b, C * b + C), (lst, c0 // 16, (c0 + n) // 16))

    order1 = [k for call in PLAN["send"][0] for k in call]
    mine = PLAN["mine"][0]
    for i, k in enumerate(order1):
        for b in range(4):
            if b not in mine[i]:
                move("s", "ft", "xp", "ord1", PC * (a0 ^ k), PC, b)
    for i, k in enumerate(order1):
        for j, b in enumerate(mine[i]):
            move("v", "ft", "xp", "ord1", PC * (a0 ^ k), PC, b)
            if j == 0 and i > 1:
                pack(1, order1[i - 1], "ft")
                send(1, order1[i - 1])
        if i in (0, 3):
            pack(1, k, "ft")
            send(1, k)
    emit("1", T.oa)

    spread("v")
    zero(("rv2", 127, 32 * 384, 128), 96)
    zero(("ra2", 0, 96), 96)
    zero(("rc2", 0, 4), 4)
    memset(("half", 0, 512), 0.5)
    quant("qm", 0, PC, "ms", 0)
    for b in range(4):
        quant("qe", PC * b, PC, "e%d" % (b % 2), 2 - b // 2 * 2)

    def layer(k):
        x, x0, parts = arrived(1, k)
        for b in (0, 2, 1, 3):
            mm(b, "wq", PC * b, x, x0, PC)
        for b in (0, 2, 1, 3):
            for at, c0, wd in parts:
                o, i = ("ht", 4 * c0 + b, 4 * (c0 + wd), 4), ("ps", 512 * b + at, 512 * b + at + wd)
                if b in PLAN["evac"][k]:
                    act(o, i, ACT.Copy, scale=0.00390625)
                else:
                    ts(o, i, 0.00390625, None, A.mult)
        quant("qh", PC * (a0 ^ k), PC, "ht", 4 * PC * (a0 ^ k))
        planes("hp", "ht", PC * (a0 ^ k), PC)

    sorter("2", "vb", "qh", (None, 0, None, 1), layer,
           [lambda: memset(("w2", 512, 544), 0.0), lambda: memset(("w2", 0, 16), 0.0)])

    def sort_h(q, b, c0, n):
        gather(q, ("hs", C * b + c0, C * b + c0 + n), ("hp", C * b, C * b + C), ("ord2", c0 // 16, (c0 + n) // 16))

    def run(b):
        scan(("sc", C * b, C * b + C), ("half", 0, C), ("hs", C * b, C * b + C), 0.0, A.mult, A.max)

    sort_h("s", 1, 0, C)
    sort_h("s", 2, 0, C)
    sort_h("s", 3, 256, 256)
    sort_h("v", 0, 0, C)
    sort_h("v", 3, 0, 256)
    for b in range(4):
        run(b)
    order2 = [k for call in PLAN["send"][1] for k in call]
    mine = PLAN["mine"][1]
    for i, k in enumerate(order2):
        for b in range(4):
            if b not in mine[i]:
                move("s", "tt", "sc", "plc2", PC * (a0 ^ k), PC, b)
    for i, k in enumerate(order2):
        for j, b in enumerate(mine[i]):
            move("v", "tt", "sc", "plc2", PC * (a0 ^ k), PC, b)
            if j == 0 and i > 0:
                pack(2, order2[i - 1], "tt")
                send(2, order2[i - 1])
    pack(2, order2[3], "tt")
    send(2, order2[3])
    emit("2", T.ob)

    comes = [("b" + "eo"[odd], RUN * (1 - odd), [(RUN * odd, PC * a0 + RUN * odd, RUN)])]
    for k in PLAN["home"]:
        x, x0, parts = arrived(2, k)
        comes.append((x, x0, parts if k else [parts[odd]]))
    for i, (x, x0, parts) in enumerate(comes):
        for b in range(4):
            mm(4 * (i % 2) + b, "qe", PC * b, x, x0, PC)
        for b in range(4):
            for at, c0, wd in parts:
                bank = 512 * (4 * (i % 2) + b)
                tt(("zs", C * b + c0, C * b + c0 + wd), ("ps", bank + at, bank + at + wd),
                   ("ft", 4 * c0 + b, 4 * (c0 + wd), 4), A.add)
    cuts = [0]
    for wd in PLAN["out"]:
        cuts.append(cuts[-1] + wd)
    nout = len(PLAN["out"])

    def result(h):
        lo, hi = cuts[h], cuts[h + 1]
        if h == nout - 1 and hi - lo >= 2 * PC:
            mid = (lo + hi) // 2
            mm(6, "qm", 0, "qz", lo, mid - lo)
            mm(7, "qm", 0, "qz", mid, hi - mid)
            copy(("ys", lo, mid), ("ps", 512 * 6, 512 * 6 + mid - lo))
            copy(("ys", mid, hi), ("ps", 512 * 7, 512 * 7 + hi - mid), "s")
        else:
            mm(h, "qm", 0, "qz", lo, hi - lo)
            copy(("ys", lo, hi), ("ps", 512 * h, 512 * h + hi - lo), "s")
        store("s" if h == nout - 1 else "y", T.y[:, lo:hi], T.ys[:, lo:hi], [("ys", lo, hi)])

    def close(h):
        lo, hi = cuts[h], cuts[h + 1]
        quant("qz", lo, hi - lo, "zt", 4 * lo)
        store("y", T.oc[:, 4 * lo:4 * hi], _view(T, "qzc", lo, hi), [("qzc", lo, hi)])

    for h in range(nout):
        lo, hi = cuts[h], cuts[h + 1]
        for b in ((0, 1, 2) if h == 0 else (0, 1)):
            move("s", "zt", "zs", "plc1", lo, hi - lo, b)
        if h > 1:
            result(h - 2)
        move("v", "zt", "zs", "plc1", lo, hi - lo, 3)
        if h:
            close(h - 1)
            move("v", "zt", "zs", "plc1", lo, hi - lo, 2)
    if nout > 1:
        result(nout - 2)
    close(nout - 1)
    for k in range(4):
        store("ys"[k % 2], T.osc[4 * k:4 * k + 4, :], T.qzs[32 * k:32 * k + 4, :], [("qzs", 0, C)])
    result(nout - 1)

    for sem, n in count.items():
        if n:
            wait("g", sem, n)
